import numpy as np
import ml_dtypes


def mxq(x, axis, fmt="e4m3"):
    dtype, down = {"e4m3": (ml_dtypes.float8_e4m3fn, 7), "e5m2": (ml_dtypes.float8_e5m2, 14)}[fmt]
    v = np.moveaxis(np.asarray(x, np.float32).astype(ml_dtypes.bfloat16).astype(np.float64), axis, -1)
    blocks = v.reshape(v.shape[:-1] + (-1, 32))
    amax = np.abs(blocks).max(-1, keepdims=True)
    byte = np.maximum(np.where(amax > 0, np.frexp(amax)[1] - 1 + 127, 0) - down, 1)
    scale = np.exp2(byte - 127.0)
    codes = (blocks / scale).astype(np.float32).astype(dtype).astype(np.float64)
    return np.moveaxis((codes * scale).reshape(v.shape), -1, axis)


WIDE = False


def mx_kscale(k):
    if not WIDE:
        return np.ones(k)
    levels = np.array([10, -10, 5, -5, 0])
    if k % 512:
        return np.exp2(np.random.permutation(np.resize(levels, k // 32))).repeat(32)
    a = np.empty((k // 512, 16))
    for p in range(k // 512):
        a[p, :8] = np.random.permutation(np.resize(levels, 8))
        for g in range(8):
            far = levels[np.abs(levels - a[p, g]) >= 10]
            a[p, g + 8] = far[np.random.randint(len(far))]
    return np.exp2(a.ravel()).repeat(32)


def f64(x):
    return np.asarray(x).astype(np.float64)


def striped(idx):
    return np.tile(idx.reshape(-1, 16).T, (8, 1)).astype(np.uint16)


def unstriped(offs):
    return offs[:16].T.reshape(-1).astype(np.int64)


E2M1 = np.array([0.0, 0.5, 1.0, 1.5, 2.0, 3.0, 4.0, 6.0, -0.0, -0.5, -1.0, -1.5, -2.0, -3.0, -4.0, -6.0])


def pack_weight(w, fmt):
    k, n = w.shape
    w = f64(np.asarray(w, np.float32).astype(ml_dtypes.bfloat16)).reshape(k // 32, 32, n)
    amax = np.abs(w).max(1)
    if fmt == "e4m3":
        byte = np.frexp(amax)[1] - 1 + 127 - 7
    else:
        mant, ex = np.frexp(amax / 6.0)
        byte = np.where(mant > 0.5, ex, ex - 1) + 127
    byte = np.clip(np.where(amax > 0, byte, 1), 1, 254)
    scaled = (w * np.exp2(127.0 - byte)[:, None, :]).reshape(k, n).astype(np.float32)
    by_word = np.ascontiguousarray(scaled.reshape(k // 512, 128, 4, n).transpose(0, 1, 3, 2))
    if fmt == "e4m3":
        words = by_word.astype(ml_dtypes.float8_e4m3fn).view(np.uint8)
    else:
        c = by_word.astype(ml_dtypes.float4_e2m1fn).view(np.uint8) & 0xF
        words = (c[..., 0::2] | (c[..., 1::2] << 4)).reshape(k // 512, 128, 2 * n)
    return np.ascontiguousarray(words), np.ascontiguousarray(byte.astype(np.uint8).reshape(k // 512, 16, n))


def unpack_weight(words, scales, fmt):
    g, _, n = scales.shape
    words = np.ascontiguousarray(words).reshape(g, 128, n, -1)
    if fmt == "e4m3":
        vals = words.view(ml_dtypes.float8_e4m3fn).astype(np.float64)
    else:
        nib = np.empty((g, 128, n, 4), np.uint8)
        nib[..., 0::2] = words & 0xF
        nib[..., 1::2] = words >> 4
        vals = E2M1[nib]
    vals = vals * np.repeat(np.exp2(scales.astype(np.float64) - 127.0), 8, axis=1)[..., None]
    return vals.transpose(0, 1, 3, 2).reshape(g * 512, n)


def gelu(v):
    return 0.5 * v * (1.0 + np.tanh(np.sqrt(2.0 / np.pi) * (v + 0.044715 * v**3)))


def bf(x):
    return np.asarray(x, np.float32).astype(ml_dtypes.bfloat16)


def planes(Y):
    n, m = Y.shape
    b = f64(bf(Y)).reshape(n // 32, 32, m)
    amax = np.abs(b).max(1)
    byte = np.clip(np.where(amax > 0, np.frexp(amax)[1] - 1 + 127 - 7, 1), 1, 254)
    codes = (b * np.exp2(127.0 - byte)[:, None, :]).reshape(n, m).astype(np.float32).astype(ml_dtypes.float8_e4m3fn).view(np.uint8)
    words = codes.reshape(n // 512, 128, 4, m).transpose(0, 1, 3, 2)
    return np.ascontiguousarray(words), np.ascontiguousarray(byte.astype(np.uint8).reshape(n // 512, 16, m))


K, T, S, T2, H, N = 1024, 4096, 1024, 2048, 512, 384

def setup_inputs():
    n = np.random.standard_normal
    s = mx_kscale(K)[:, None]
    u = mx_kscale(H)[:, None]
    tab_words, tab_scales = pack_weight(n((K, T)) * s, "e4m3")
    w2_words, w2_scales = pack_weight(n((H, H)) / np.sqrt(H) / u * u.T, "e2m1")
    return {
        "tab_words": tab_words, "tab_scales": tab_scales,
        "offs": striped(np.random.permutation(T)[:S]),
        "offs2": striped(np.random.permutation(T2)[:S]),
        "w1": (n((K, H)) / np.sqrt(K) / s).astype(np.float32),
        "gain": (1.5 * np.exp(0.3 * n(H)) * u[:, 0]).astype(np.float32),
        "w2_words": w2_words, "w2_scales": w2_scales,
        "res": (np.random.uniform(0.5, 1.5, H) * u[:, 0]).astype(np.float32),
        "wgs": np.exp(0.3 * n((128, S))).astype(np.float32),
        "page0": (n((H, T2)) * u).astype(np.float32),
        "w3": (n((H, N)) / np.sqrt(H) / u).astype(np.float32),
        "anchor": n((N, T2)).astype(np.float32),
    }

def reference(tab_words, tab_scales, offs, offs2, w1, gain, w2_words, w2_scales, res, wgs, page0, w3, anchor):
    v = unpack_weight(tab_words, tab_scales, "e4m3")[:, unstriped(offs)]
    base = mxq(f64(w1), 0, "e4m3").T @ v
    gel = 0.5 * base * (1.0 + np.tanh(0.7978845608028654 * (base + 0.044715 * base ** 3)))
    act = f64(gain)[:, None] * gel
    further = unpack_weight(w2_words, w2_scales, "e2m1").T @ mxq(act, 0, "e4m3")
    h = f64(res)[:, None] * base + further
    page = f64(page0).copy()
    page[:, unstriped(offs2)] = np.tile(f64(wgs), (H // 128, 1)) * h
    y = (mxq(f64(w3), 0, "e4m3").T @ mxq(page, 0, "e4m3")) - f64(anchor)
    words, scales = planes(page)
    return y, page, words, scales

@@ -1,0 +1,343 @@
+from contextlib import ExitStack
+
+import concourse.mybir as mybir
+
+K, T, S, T2, H, N = 1024, 4096, 1024, 2048, 512, 384
+FLOPS = 2 * (K * H * S + H * H * S + H * N * T2)
+
+F32 = mybir.dt.float32
+BF16 = mybir.dt.bfloat16
+I32 = mybir.dt.int32
+U32 = mybir.dt.uint32
+U16 = mybir.dt.uint16
+U8 = mybir.dt.uint8
+FP8X4 = mybir.dt.float8_e4m3fn_x4
+FP4X4 = mybir.dt.float4_e2m1fn_x4
+MULT = mybir.AluOpType.mult
+ADD = mybir.AluOpType.add
+SUB = mybir.AluOpType.subtract
+GELU = mybir.ActivationFunctionType.Gelu_apprx_tanh
+COPY = mybir.ActivationFunctionType.Copy
+
+P = 128
+PACK = 4
+PASSES = K // (P * PACK)
+BANK = 512
+HALF = S // 2
+TOKEN_CHUNKS = ((0, 256), (256, 256), (512, 512))
+PAGE_CHUNKS = ((0, 256), (256, 256), (512, 512), (1024, 512), (1536, 512))
+QUADRANT_ORDER = (0, 2, 1, 3)
+
+
+def tile_list_rubric_prefix_cache_kernel(
+    tc, tab_words, tab_scales, offs, offs2, w1, gain, w2_words, w2_scales, res, wgs, page0, w3, anchor,
+    out_0, out_1, out_2, out_3,
+):
+    nc = tc.nc
+    with ExitStack() as ctx:
+        lists = ctx.enter_context(tc.tile_pool(name="lists", bufs=1))
+        sb = ctx.enter_context(tc.tile_pool(name="sb", bufs=1))
+        psum = ctx.enter_context(tc.psum_pool(name="psum", bufs=1))
+
+        def tile(shape, dtype, name, tag=None, bufs=1):
+            return sb.tile(shape, dtype, name=name, tag=tag or name, bufs=bufs, align_bytes=64)
+
+        def bank(index, name):
+            return psum.tile([P, BANK], F32, name=name, tag="bank%d" % index)
+
+        idx = lists.tile([P, S // 16], U16, name="idx")
+        idx2 = lists.tile([P, S // 16], U16, name="idx2")
+        w2w_raw = tile([P, 2 * H], U8, "w2w_raw", tag="wide0")
+        nc.sync.dma_start(w2w_raw[:].bitcast(I32), w2_words[0].bitcast(I32))
+        w1_raw = tile([P, PASSES, PACK, H], F32, "w1_raw", tag="wide1")
+        nc.sync.dma_start(w1_raw[:], w1.rearrange("(a p j) r -> p a j r", a=PASSES, j=PACK))
+        nc.sync.dma_start(idx[:], offs)
+        nc.sync.dma_start(idx2[:], offs2)
+
+        tabs = tile([P, T], U8, "tabs")
+        nc.vector.memset(tabs[:].bitcast(I32), 0)
+        for q in QUADRANT_ORDER:
+            nc.scalar.dma_start(
+                tabs[32 * q : 32 * q + 4 * PASSES, :].bitcast(I32), tab_scales[:, 4 * q : 4 * q + 4, :].bitcast(I32)
+            )
+
+        w2s_raw = tile([P, H], U8, "w2s_raw")
+        gain_t = tile([P, PACK], F32, "gain_t")
+        res_t = tile([P, PACK], F32, "res_t")
+        nc.gpsimd.memset(w2s_raw[:].bitcast(I32), 0)
+        for q in range(4):
+            nc.gpsimd.dma_start(w2s_raw[32 * q : 32 * q + 4, :].bitcast(I32), w2_scales[0, 4 * q : 4 * q + 4, :].bitcast(I32))
+        nc.gpsimd.dma_start(gain_t[:], gain.rearrange("(p t) -> p t", t=PACK))
+        nc.gpsimd.dma_start(res_t[:], res.rearrange("(p t) -> p t", t=PACK))
+
+        w2w = tile([P, 2 * H], U8, "w2w")
+        nc.vector.tensor_copy(
+            w2w[:].rearrange("p (t m b) -> p t m b", t=PACK, b=2), w2w_raw[:].rearrange("p (m t b) -> p t m b", t=PACK, b=2)
+        )
+
+        w1c = [tile([P, H], U32, "w1c%d" % a) for a in range(PASSES)]
+        w1s = [tile([P, H], U8, "w1s%d" % a) for a in range(PASSES)]
+        for a in range(PASSES):
+            w1_bf = tile([P, H * PACK], BF16, "w1_bf%d" % a)
+            dealt = w1_bf[:].rearrange("p (t m j) -> p m t j", t=PACK, j=PACK)
+            rows = w1_raw[:, a].rearrange("p j (m t) -> p m t j", t=PACK)
+            cut = (P, 40)[a]
+            nc.vector.tensor_copy(dealt[:, 0:cut], rows[:, 0:cut])
+            if cut < P:
+                nc.scalar.copy(dealt[:, cut:P], rows[:, cut:P])
+            nc.vector.quantize_mx(out=w1c[a][:].bitcast(FP8X4), scales=w1s[a][:], in_=w1_bf[:])
+
+        tabw = [tile([P, T], U32, "tabw%d" % a, tag="wide%d" % a) for a in range(PASSES)]
+        for a in range(PASSES):
+            nc.sync.dma_start(tabw[a][:].bitcast(I32), tab_words[a].rearrange("p t i -> p (t i)").bitcast(I32))
+
+        vs = tile([P, S], U8, "vs")
+        nc.vector.tensor_copy(vs[:], tabs[:].indirect(idx[:]))
+        vw = {}
+        for a in range(PASSES):
+            vw[a] = tile([P, S], U32, "vw%d" % a, tag=("tabs", "wide0")[a])
+            for j0 in (0, HALF):
+                nc.vector.tensor_copy(vw[a][:, j0 : j0 + HALF], tabw[a][:].indirect(idx[:, j0 // 16 : (j0 + HALF) // 16]))
+
+        w2s = tile([P, H], U8, "w2s", tag="w1_bf0")
+        nc.vector.tensor_copy(w2s[:].rearrange("p (t m) -> p t m", t=PACK), w2s_raw[:].rearrange("p (m t) -> p t m", t=PACK))
+        page = {}
+        page0_rows = page0.rearrange("(p t) m -> t p m", t=PACK)
+        wgs_rows = wgs.rearrange("(q t) j -> q t j", t=PACK)
+        wgs_c = {}
+
+        def load_wgs(c, tag):
+            j0, n = TOKEN_CHUNKS[c]
+            wgs_c[c] = tile([P, PACK, n], F32, "wgs%d" % c, tag=tag)
+            for q in QUADRANT_ORDER:
+                nc.sync.dma_start(wgs_c[c][32 * q : 32 * q + 32], wgs_rows[:, :, j0 : j0 + n])
+
+        def load_page(t, tag):
+            page[t] = tile([P, T2], F32, "page%d" % t, tag=tag)
+            nc.sync.dma_start(page[t][:], page0_rows[t])
+
+        load_page(0, "w2s_raw")
+        load_wgs(0, "w1_bf1")
+        load_page(1, "wide1")
+
+        base, fur, rb, h, actc, acts, act_bf = {}, {}, {}, {}, {}, {}, {}
+
+        def mm1(c, t, a):
+            j0, n = TOKEN_CHUNKS[c]
+            cols = slice(t * P, (t + 1) * P)
+            nc.tensor.matmul_mx(
+                out=base[c, t],
+                lhsT=w1c[a][:, cols].bitcast(FP8X4),
+                lhsT_scale=w1s[a][:, cols],
+                rhs=vw[a][:, j0 : j0 + n].bitcast(FP8X4),
+                rhs_scale=vs[4 * a : P, j0 : j0 + n],
+                start=(a == 0),
+                stop=(a == PASSES - 1),
+            )
+
+        def gelu(c, t):
+            n = TOKEN_CHUNKS[c][1]
+            first = (c, t) == (0, 0)
+            g = tile([P, n], F32, "g%d_%d" % (c, t), tag="g_first" if first else "g", bufs=1 if first else 4)
+            nc.scalar.activation(g[:], base[c, t], GELU)
+            return g
+
+        def residual(c, t):
+            n = TOKEN_CHUNKS[c][1]
+            rb[c, t] = tile([P, n], F32, "rb%d_%d" % (c, t))
+            nc.scalar.activation(rb[c, t][:], base[c, t], COPY, scale=res_t[:, t : t + 1])
+
+        def act_on_scalar(c):
+            n = TOKEN_CHUNKS[c][1]
+            rows = tile([P, PACK, n], BF16, "act_rows%d" % c, tag="act_rows")
+            gs = [gelu(c, t) for t in range(PACK)]
+            for t in range(PACK):
+                nc.scalar.activation(rows[:, t, :], gs[t][:], COPY, scale=gain_t[:, t : t + 1])
+            act_bf[c] = tile([P, n * PACK], BF16, "act_bf%d" % c, tag="hold%d" % c)
+            nc.scalar.copy(
+                act_bf[c][:].rearrange("p (g i t) -> p g t i", i=4, t=PACK),
+                rows[:].rearrange("p t (g i) -> p g t i", i=4),
+            )
+
+        def quant_act(c):
+            n = TOKEN_CHUNKS[c][1]
+            actc[c] = tile([P, n], U32, "actc%d" % c)
+            acts[c] = tile([P, n], U8, "acts%d" % c)
+            nc.vector.quantize_mx(out=actc[c][:].bitcast(FP8X4), scales=acts[c][:], in_=act_bf[c][:])
+
+        def mm2(c, t, b):
+            n = TOKEN_CHUNKS[c][1]
+            fur[c, t] = bank(b, "fur%d_%d" % (c, t))[:, 0:n]
+            nc.tensor.matmul_mx(
+                out=fur[c, t],
+                lhsT=w2w[:, 2 * t * P : 2 * (t + 1) * P].bitcast(FP4X4),
+                lhsT_scale=w2s[:, t * P : (t + 1) * P],
+                rhs=actc[c][:].bitcast(FP8X4),
+                rhs_scale=acts[c][:],
+                start=True,
+                stop=True,
+            )
+
+        def add(c, t, dst):
+            h[c, t] = dst
+            nc.vector.tensor_tensor(dst, fur[c, t], rb[c, t][:], ADD)
+
+        def scatter(c, t):
+            j0, n = TOKEN_CHUNKS[c]
+            nc.vector.tensor_tensor(
+                page[t][:].indirect(idx2[:, j0 // 16 : (j0 + n) // 16]), h[c, t], wgs_c[c][:, t, :], MULT
+            )
+
+        def h_tile(c, t, tag=None):
+            return tile([P, TOKEN_CHUNKS[c][1]], F32, "h%d_%d" % (c, t), tag=tag)[:]
+
+        for t in range(PACK):
+            base[0, t] = bank(t, "base0_%d" % t)[:, 0:256]
+        for a in range(PASSES):
+            for t in range(PACK):
+                mm1(0, t, a)
+        act_bf[0] = tile([P, 256 * PACK], BF16, "act_bf0")
+        for t in range(PACK):
+            g = gelu(0, t)
+            nc.vector.tensor_scalar(
+                act_bf[0][:].rearrange("p (n t) -> p t n", t=PACK)[:, t, :], g[:], gain_t[:, t : t + 1], None, MULT
+            )
+        quant_act(0)
+        load_page(2, "g_first")
+        load_page(3, "act_bf0")
+        residual(0, 0)
+        residual(0, 1)
+        mm2(0, 0, 6)
+        mm2(0, 1, 7)
+        for pair in range(2):
+            both = bank(4 + pair, "base1_%d" % pair)
+            for t in (2 * pair, 2 * pair + 1):
+                base[1, t] = both[:, (t % 2) * 256 : (t % 2 + 1) * 256]
+                for a in range(PASSES):
+                    mm1(1, t, a)
+        add(0, 0, h_tile(0, 0))
+        add(0, 1, h_tile(0, 1))
+        scatter(0, 0)
+        scatter(0, 1)
+        act_on_scalar(1)
+        quant_act(1)
+        residual(0, 2)
+        residual(0, 3)
+        mm2(0, 2, 6)
+        mm2(0, 3, 7)
+        held = tile([P, 2, 256], F32, "h0_23", tag="hold1")
+        add(0, 2, held[:, 0, :])
+        add(0, 3, held[:, 1, :])
+        scatter(0, 2)
+        for t in range(PACK - 1):
+            residual(1, t)
+        for t in range(PACK):
+            base[2, t] = bank(t, "base2_%d" % t)[:]
+            for a in range(PASSES):
+                mm1(2, t, a)
+        load_wgs(1, "tabs")
+        load_wgs(2, "wide0")
+        w3_raw = tile([P, PACK, N], F32, "w3_raw", tag="rb0_3")
+        nc.sync.dma_start(w3_raw[:], w3.rearrange("(p j) n -> p j n", j=PACK))
+        for t in range(PACK - 1):
+            mm2(1, t, (4, 6, 7)[t])
+        add(1, 0, h_tile(1, 0))
+        add(1, 1, h_tile(1, 1))
+        scatter(0, 3)
+        scatter(1, 0)
+        add(1, 2, h_tile(1, 2))
+        scatter(1, 1)
+        scatter(1, 2)
+        anchor_rows = anchor.rearrange("(j p) m -> p j m", p=P)
+        anc_tags = ("hold1", "rb1_0", "rb1_1", "rb1_2", "h1_0")
+        anc = []
+        for k, (m0, w) in enumerate(PAGE_CHUNKS):
+            anc.append(tile([P, N // P, w], F32, "anc%d" % k, tag=anc_tags[k]))
+            nc.sync.dma_start(anc[k][:], anchor_rows[:, :, m0 : m0 + w])
+        act_on_scalar(2)
+        quant_act(2)
+        residual(1, 3)
+        mm2(1, 3, 5)
+        add(1, 3, h_tile(1, 3, tag="hold2"))
+        for t in range(PACK):
+            residual(2, t)
+        for t in range(PACK):
+            mm2(2, t, (4, 6, 7, 5)[t])
+        add(2, 0, h_tile(2, 0))
+        add(2, 1, h_tile(2, 1))
+        scatter(1, 3)
+
+        w3_bf = tile([P, N * PACK], BF16, "w3_bf")
+        nc.scalar.copy(w3_bf[:].rearrange("p (n j) -> p n j", j=PACK), w3_raw[:].rearrange("p j n -> p n j"))
+
+        out1_rows = out_1.rearrange("(p t) m -> t p m", t=PACK)
+        rounded = [tile([P, PACK, w], BF16, "rounded%d" % k) for k, (m0, w) in enumerate(PAGE_CHUNKS)]
+
+        def round_page(k, t):
+            m0, w = PAGE_CHUNKS[k]
+            nc.scalar.copy(rounded[k][:, t, :], page[t][:, m0 : m0 + w])
+
+        for t in range(PACK):
+            scatter(2, t)
+            if t + 2 < PACK:
+                add(2, t + 2, h_tile(2, t + 2, tag="h2_%d" % (t + 2)))
+            nc.sync.dma_start(out1_rows[t], page[t][:])
+            if t < PACK - 1:
+                for k in range(len(PAGE_CHUNKS)):
+                    round_page(k, t)
+
+        w3c = tile([P, N], U32, "w3c", tag="h2_3")
+        w3s = tile([P, N], U8, "w3s")
+        for n0, n1 in ((0, 256), (256, N)):
+            nc.vector.quantize_mx(
+                out=w3c[:, n0:n1].bitcast(FP8X4), scales=w3s[:, n0:n1], in_=w3_bf[:, n0 * PACK : n1 * PACK]
+            )
+
+        pscale = tile([P, T2], U8, "pscale")
+        out0_rows = out_0.rearrange("(j p) m -> p j m", p=P)
+        out2_words = out_2[0].rearrange("p m t -> p (m t)").bitcast(I32)
+        pcode = {}
+
+        def quant_page(k):
+            m0, w = PAGE_CHUNKS[k]
+            round_page(k, PACK - 1)
+            page_bf = tile([P, w * PACK], BF16, "page_bf%d" % k, tag="page_bf", bufs=3)
+            (nc.vector.tensor_copy if k < 2 else nc.scalar.copy)(
+                page_bf[:].rearrange("p (g i t) -> p g t i", i=4, t=PACK),
+                rounded[k][:].rearrange("p t (g i) -> p g t i", i=4),
+            )
+            pcode[k] = tile([P, w], U32, "pcode%d" % k, tag=anc_tags[k - 2] if k >= 2 else None)
+            nc.vector.quantize_mx(out=pcode[k][:].bitcast(FP8X4), scales=pscale[:, m0 : m0 + w], in_=page_bf[:])
+            nc.sync.dma_start(out2_words[:, m0 : m0 + w], pcode[k][:].bitcast(I32))
+
+        def features(k):
+            m0, w = PAGE_CHUNKS[k]
+            dst = tile([P, N // P, w], F32, "feat%d" % k)
+            last = k == len(PAGE_CHUNKS) - 1
+            for j in range(N // P):
+                y = bank((3 * k + j) % 8, "y%d_%d" % (k, j))[:, 0:w]
+                nc.tensor.matmul_mx(
+                    out=y,
+                    lhsT=w3c[:, j * P : (j + 1) * P].bitcast(FP8X4),
+                    lhsT_scale=w3s[:, j * P : (j + 1) * P],
+                    rhs=pcode[k][:].bitcast(FP8X4),
+                    rhs_scale=pscale[:, m0 : m0 + w],
+                    start=True,
+                    stop=True,
+                )
+                nc.vector.tensor_tensor(dst[:, j, :], y, anc[k][:, j, :], SUB)
+                if last:
+                    nc.sync.dma_start(out0_rows[:, j, m0 : m0 + w], dst[:, j, :])
+            if not last:
+                nc.sync.dma_start(out0_rows[:, :, m0 : m0 + w], dst[:])
+
+        quant_page(0)
+        for k in range(len(PAGE_CHUNKS)):
+            if k + 1 < len(PAGE_CHUNKS):
+                quant_page(k + 1)
+            else:
+                for q in range(4):
+                    nc.scalar.dma_start(
+                        out_3[0, 4 * q : 4 * q + 4, :].bitcast(I32), pscale[32 * q : 32 * q + 4, :].bitcast(I32)
+                    )
+            features(k)

@@ -104,20 +104,21 @@ def tile_list_rubric_prefix_cache_kernel(
         page = {}
         page0_rows = page0.rearrange("(p t) m -> t p m", t=PACK)
         wgs_rows = wgs.rearrange("(q t) j -> q t j", t=PACK)
-        wgs_c = {}
+        wgs_t = {}
 
-        def load_wgs(c, tag):
-            j0, n = TOKEN_CHUNKS[c]
-            wgs_c[c] = tile([P, PACK, n], F32, "wgs%d" % c, tag=tag)
+        def load_wgs(half, t0, t1, tag):
+            part = tile([P, t1 - t0, HALF], F32, "wgs%d_%d" % (half, t0), tag=tag)
             for q in QUADRANT_ORDER:
-                nc.sync.dma_start(wgs_c[c][32 * q : 32 * q + 32], wgs_rows[:, :, j0 : j0 + n])
+                nc.sync.dma_start(part[32 * q : 32 * q + 32], wgs_rows[:, t0:t1, half * HALF : (half + 1) * HALF])
+            for t in range(t0, t1):
+                wgs_t[half, t] = part[:, t - t0, :]
 
         def load_page(t, tag):
             page[t] = tile([P, T2], F32, "page%d" % t, tag=tag)
             nc.sync.dma_start(page[t][:], page0_rows[t])
 
+        load_wgs(0, 0, 2, "w1_bf1")
         load_page(0, "w2s_raw")
-        load_wgs(0, "w1_bf1")
         load_page(1, "wide1")
 
         base, fur, rb, h, actc, acts, act_bf = {}, {}, {}, {}, {}, {}, {}
@@ -137,15 +138,14 @@ def tile_list_rubric_prefix_cache_kernel(
 
         def gelu(c, t):
             n = TOKEN_CHUNKS[c][1]
-            first = (c, t) == (0, 0)
-            g = tile([P, n], F32, "g%d_%d" % (c, t), tag="g_first" if first else "g", bufs=1 if first else 4)
+            g = tile([P, n], F32, "g%d_%d" % (c, t), tag="g" if c else None, bufs=4 if c else 1)
             nc.scalar.activation(g[:], base[c, t], GELU)
             return g
 
-        def residual(c, t):
+        def residual(c, t, dst=None):
             n = TOKEN_CHUNKS[c][1]
-            rb[c, t] = tile([P, n], F32, "rb%d_%d" % (c, t))
-            nc.scalar.activation(rb[c, t][:], base[c, t], COPY, scale=res_t[:, t : t + 1])
+            rb[c, t] = tile([P, n], F32, "rb%d_%d" % (c, t))[:] if dst is None else dst
+            nc.scalar.activation(rb[c, t], base[c, t], COPY, scale=res_t[:, t : t + 1])
 
         def act_on_scalar(c):
             n = TOKEN_CHUNKS[c][1]
@@ -180,13 +180,15 @@ def tile_list_rubric_prefix_cache_kernel(
 
         def add(c, t, dst):
             h[c, t] = dst
-            nc.vector.tensor_tensor(dst, fur[c, t], rb[c, t][:], ADD)
+            nc.vector.tensor_tensor(dst, fur[c, t], rb[c, t], ADD)
+
+        def scatter_span(t, j0, n, values):
+            weights = wgs_t[j0 // HALF, t][:, j0 % HALF : j0 % HALF + n]
+            nc.vector.tensor_tensor(page[t][:].indirect(idx2[:, j0 // 16 : (j0 + n) // 16]), values, weights, MULT)
 
         def scatter(c, t):
             j0, n = TOKEN_CHUNKS[c]
-            nc.vector.tensor_tensor(
-                page[t][:].indirect(idx2[:, j0 // 16 : (j0 + n) // 16]), h[c, t], wgs_c[c][:, t, :], MULT
-            )
+            scatter_span(t, j0, n, h[c, t])
 
         def h_tile(c, t, tag=None):
             return tile([P, TOKEN_CHUNKS[c][1]], F32, "h%d_%d" % (c, t), tag=tag)[:]
@@ -203,12 +205,13 @@ def tile_list_rubric_prefix_cache_kernel(
                 act_bf[0][:].rearrange("p (n t) -> p t n", t=PACK)[:, t, :], g[:], gain_t[:, t : t + 1], None, MULT
             )
         quant_act(0)
-        load_page(2, "g_first")
-        load_page(3, "act_bf0")
-        residual(0, 0)
-        residual(0, 1)
-        mm2(0, 0, 6)
-        mm2(0, 1, 7)
+        load_wgs(0, 2, 4, "g0_0")
+        load_page(2, "g0_1")
+        load_page(3, "g0_2")
+        load_wgs(1, 0, 4, "g0_3")
+        for t in range(2):
+            residual(0, t)
+            mm2(0, t, t)
         for pair in range(2):
             both = bank(4 + pair, "base1_%d" % pair)
             for t in (2 * pair, 2 * pair + 1):
@@ -221,35 +224,35 @@ def tile_list_rubric_prefix_cache_kernel(
         scatter(0, 1)
         act_on_scalar(1)
         quant_act(1)
-        residual(0, 2)
-        residual(0, 3)
+        residual(1, 0)
+        residual(1, 1)
+        rb_late = tile([P, 2, 256], F32, "rb0_23", tag="act_bf0")
+        residual(0, 2, rb_late[:, 0, :])
+        residual(0, 3, rb_late[:, 1, :])
         mm2(0, 2, 6)
         mm2(0, 3, 7)
-        held = tile([P, 2, 256], F32, "h0_23", tag="hold1")
+        held = tile([P, 3, 256], F32, "h_held", tag="hold1")
         add(0, 2, held[:, 0, :])
-        add(0, 3, held[:, 1, :])
-        scatter(0, 2)
-        for t in range(PACK - 1):
-            residual(1, t)
+        add(0, 3, held[:, 2, :])
+        mm2(1, 0, 4)
+        mm2(1, 1, 6)
         for t in range(PACK):
             base[2, t] = bank(t, "base2_%d" % t)[:]
             for a in range(PASSES):
                 mm1(2, t, a)
-        load_wgs(1, "tabs")
-        load_wgs(2, "wide0")
-        w3_raw = tile([P, PACK, N], F32, "w3_raw", tag="rb0_3")
+        w3_raw = tile([P, PACK, N], F32, "w3_raw", tag="tabs")
         nc.sync.dma_start(w3_raw[:], w3.rearrange("(p j) n -> p j n", j=PACK))
-        for t in range(PACK - 1):
-            mm2(1, t, (4, 6, 7)[t])
         add(1, 0, h_tile(1, 0))
         add(1, 1, h_tile(1, 1))
-        scatter(0, 3)
         scatter(1, 0)
-        add(1, 2, h_tile(1, 2))
+        residual(1, 2)
+        mm2(1, 2, 4)
+        add(1, 2, held[:, 1, :])
         scatter(1, 1)
-        scatter(1, 2)
+        scatter_span(2, 0, HALF, held[:, 0:2, :].rearrange("p c n -> p (c n)"))
+        scatter(0, 3)
         anchor_rows = anchor.rearrange("(j p) m -> p j m", p=P)
-        anc_tags = ("hold1", "rb1_0", "rb1_1", "rb1_2", "h1_0")
+        anc_tags = ("rb1_0", "rb1_1", "rb1_2", "h1_0", "h1_1")
         anc = []
         for k, (m0, w) in enumerate(PAGE_CHUNKS):
             anc.append(tile([P, N // P, w], F32, "anc%d" % k, tag=anc_tags[k]))
@@ -267,9 +270,6 @@ def tile_list_rubric_prefix_cache_kernel(
         add(2, 1, h_tile(2, 1))
         scatter(1, 3)
 
-        w3_bf = tile([P, N * PACK], BF16, "w3_bf")
-        nc.scalar.copy(w3_bf[:].rearrange("p (n j) -> p n j", j=PACK), w3_raw[:].rearrange("p j n -> p n j"))
-
         out1_rows = out_1.rearrange("(p t) m -> t p m", t=PACK)
         rounded = [tile([P, PACK, w], BF16, "rounded%d" % k) for k, (m0, w) in enumerate(PAGE_CHUNKS)]
 
@@ -285,6 +285,9 @@ def tile_list_rubric_prefix_cache_kernel(
             if t < PACK - 1:
                 for k in range(len(PAGE_CHUNKS)):
                     round_page(k, t)
+            if t == 0:
+                w3_bf = tile([P, N * PACK], BF16, "w3_bf", tag="h2_0")
+                nc.scalar.copy(w3_bf[:].rearrange("p (n j) -> p n j", j=PACK), w3_raw[:].rearrange("p j n -> p n j"))
 
         w3c = tile([P, N], U32, "w3c", tag="h2_3")
         w3s = tile([P, N], U8, "w3s")
@@ -335,9 +338,9 @@ def tile_list_rubric_prefix_cache_kernel(
         for k in range(len(PAGE_CHUNKS)):
             if k + 1 < len(PAGE_CHUNKS):
                 quant_page(k + 1)
-            else:
+            if k + 2 == len(PAGE_CHUNKS):
                 for q in range(4):
-                    nc.scalar.dma_start(
+                    nc.sync.dma_start(
                         out_3[0, 4 * q : 4 * q + 4, :].bitcast(I32), pscale[32 * q : 32 * q + 4, :].bitcast(I32)
                     )
             features(k)

@@ -56,15 +56,16 @@ def tile_list_rubric_prefix_cache_kernel(
 
         tabs = tile([P, T], U8, "tabs")
         nc.vector.memset(tabs[:].bitcast(I32), 0)
-        for q in QUADRANT_ORDER:
-            nc.scalar.dma_start(
-                tabs[32 * q : 32 * q + 4 * PASSES, :].bitcast(I32), tab_scales[:, 4 * q : 4 * q + 4, :].bitcast(I32)
-            )
+        for a in range(PASSES):
+            for q in QUADRANT_ORDER:
+                (nc.scalar, nc.gpsimd)[a].dma_start(
+                    tabs[32 * q + 4 * a : 32 * q + 4 * a + 4, :].bitcast(I32), tab_scales[a, 4 * q : 4 * q + 4, :].bitcast(I32)
+                )
 
         w2s_raw = tile([P, H], U8, "w2s_raw")
         gain_t = tile([P, PACK], F32, "gain_t")
         res_t = tile([P, PACK], F32, "res_t")
-        nc.gpsimd.memset(w2s_raw[:].bitcast(I32), 0)
+        nc.vector.memset(w2s_raw[:].bitcast(I32), 0)
         for q in range(4):
             nc.gpsimd.dma_start(w2s_raw[32 * q : 32 * q + 4, :].bitcast(I32), w2_scales[0, 4 * q : 4 * q + 4, :].bitcast(I32))
         nc.gpsimd.dma_start(gain_t[:], gain.rearrange("(p t) -> p t", t=PACK))
@@ -155,8 +156,7 @@ def tile_list_rubric_prefix_cache_kernel(
                 nc.scalar.activation(rows[:, t, :], gs[t][:], COPY, scale=gain_t[:, t : t + 1])
             act_bf[c] = tile([P, n * PACK], BF16, "act_bf%d" % c, tag="hold%d" % c)
             nc.scalar.copy(
-                act_bf[c][:].rearrange("p (g i t) -> p g t i", i=4, t=PACK),
-                rows[:].rearrange("p t (g i) -> p g t i", i=4),
+                act_bf[c][:].rearrange("p (n t) -> p n t", t=PACK), rows[:].rearrange("p t n -> p n t")
             )
 
         def quant_act(c):
@@ -300,22 +300,29 @@ def tile_list_rubric_prefix_cache_kernel(
         out0_rows = out_0.rearrange("(j p) m -> p j m", p=P)
         out2_words = out_2[0].rearrange("p m t -> p (m t)").bitcast(I32)
         pcode = {}
+        pcode_head = tile([P, BANK], U32, "pcode_head")
+        feat_head = tile([P, N // P, BANK], F32, "feat_head")
 
         def quant_page(k):
             m0, w = PAGE_CHUNKS[k]
             round_page(k, PACK - 1)
             page_bf = tile([P, w * PACK], BF16, "page_bf%d" % k, tag="page_bf", bufs=3)
             (nc.vector.tensor_copy if k < 2 else nc.scalar.copy)(
-                page_bf[:].rearrange("p (g i t) -> p g t i", i=4, t=PACK),
-                rounded[k][:].rearrange("p t (g i) -> p g t i", i=4),
+                page_bf[:].rearrange("p (m t) -> p m t", t=PACK), rounded[k][:].rearrange("p t m -> p m t")
             )
-            pcode[k] = tile([P, w], U32, "pcode%d" % k, tag=anc_tags[k - 2] if k >= 2 else None)
-            nc.vector.quantize_mx(out=pcode[k][:].bitcast(FP8X4), scales=pscale[:, m0 : m0 + w], in_=page_bf[:])
-            nc.sync.dma_start(out2_words[:, m0 : m0 + w], pcode[k][:].bitcast(I32))
+            if k < 2:
+                pcode[k] = pcode_head[:, m0 : m0 + w]
+            else:
+                pcode[k] = tile([P, w], U32, "pcode%d" % k, tag=anc_tags[k - 2])[:]
+            nc.vector.quantize_mx(out=pcode[k].bitcast(FP8X4), scales=pscale[:, m0 : m0 + w], in_=page_bf[:])
+            if k == 1:
+                nc.sync.dma_start(out2_words[:, 0:BANK], pcode_head[:].bitcast(I32))
+            if k >= 2:
+                nc.sync.dma_start(out2_words[:, m0 : m0 + w], pcode[k].bitcast(I32))
 
         def features(k):
             m0, w = PAGE_CHUNKS[k]
-            dst = tile([P, N // P, w], F32, "feat%d" % k)
+            dst = feat_head[:, :, m0 : m0 + w] if k < 2 else tile([P, N // P, w], F32, "feat%d" % k)[:]
             last = k == len(PAGE_CHUNKS) - 1
             for j in range(N // P):
                 y = bank((3 * k + j) % 8, "y%d_%d" % (k, j))[:, 0:w]
@@ -323,7 +330,7 @@ def tile_list_rubric_prefix_cache_kernel(
                     out=y,
                     lhsT=w3c[:, j * P : (j + 1) * P].bitcast(FP8X4),
                     lhsT_scale=w3s[:, j * P : (j + 1) * P],
-                    rhs=pcode[k][:].bitcast(FP8X4),
+                    rhs=pcode[k].bitcast(FP8X4),
                     rhs_scale=pscale[:, m0 : m0 + w],
                     start=True,
                     stop=True,
@@ -331,8 +338,10 @@ def tile_list_rubric_prefix_cache_kernel(
                 nc.vector.tensor_tensor(dst[:, j, :], y, anc[k][:, j, :], SUB)
                 if last:
                     nc.sync.dma_start(out0_rows[:, j, m0 : m0 + w], dst[:, j, :])
-            if not last:
-                nc.sync.dma_start(out0_rows[:, :, m0 : m0 + w], dst[:])
+            if k == 1:
+                nc.sync.dma_start(out0_rows[:, :, 0:BANK], feat_head[:])
+            if k >= 2 and not last:
+                nc.sync.dma_start(out0_rows[:, :, m0 : m0 + w], dst)
 
         quant_page(0)
         for k in range(len(PAGE_CHUNKS)):

@@ -47,12 +47,15 @@ def tile_list_rubric_prefix_cache_kernel(
 
         idx = lists.tile([P, S // 16], U16, name="idx")
         idx2 = lists.tile([P, S // 16], U16, name="idx2")
-        w2w_raw = tile([P, 2 * H], U8, "w2w_raw", tag="wide0")
+        w2w_raw = tile([P, 2 * H], U8, "w2w_raw")
         nc.sync.dma_start(w2w_raw[:].bitcast(I32), w2_words[0].bitcast(I32))
-        w1_raw = tile([P, PASSES, PACK, H], F32, "w1_raw", tag="wide1")
-        nc.sync.dma_start(w1_raw[:], w1.rearrange("(a p j) r -> p a j r", a=PASSES, j=PACK))
         nc.sync.dma_start(idx[:], offs)
+        w1_raw = tile([P, PASSES, PACK, H], F32, "w1_raw")
+        nc.sync.dma_start(w1_raw[:], w1.rearrange("(a p j) r -> p a j r", a=PASSES, j=PACK))
         nc.sync.dma_start(idx2[:], offs2)
+        tabw = [tile([P, T], U32, "tabw%d" % a, tag="wide%d" % a) for a in range(PASSES)]
+        for a in range(PASSES):
+            nc.sync.dma_start(tabw[a][:].bitcast(I32), tab_words[a].rearrange("p t i -> p (t i)").bitcast(I32))
 
         tabs = tile([P, T], U8, "tabs")
         nc.vector.memset(tabs[:].bitcast(I32), 0)
@@ -88,11 +91,10 @@ def tile_list_rubric_prefix_cache_kernel(
                 nc.scalar.copy(dealt[:, cut:P], rows[:, cut:P])
             nc.vector.quantize_mx(out=w1c[a][:].bitcast(FP8X4), scales=w1s[a][:], in_=w1_bf[:])
 
-        tabw = [tile([P, T], U32, "tabw%d" % a, tag="wide%d" % a) for a in range(PASSES)]
-        for a in range(PASSES):
-            nc.sync.dma_start(tabw[a][:].bitcast(I32), tab_words[a].rearrange("p t i -> p (t i)").bitcast(I32))
+        w2s = tile([P, H], U8, "w2s", tag="w1_bf0")
+        nc.vector.tensor_copy(w2s[:].rearrange("p (t m) -> p t m", t=PACK), w2s_raw[:].rearrange("p (m t) -> p t m", t=PACK))
 
-        vs = tile([P, S], U8, "vs")
+        vs = tile([P, S], U8, "vs", tag="w2s_raw")
         nc.vector.tensor_copy(vs[:], tabs[:].indirect(idx[:]))
         vw = {}
         for a in range(PASSES):
@@ -100,26 +102,25 @@ def tile_list_rubric_prefix_cache_kernel(
             for j0 in (0, HALF):
                 nc.vector.tensor_copy(vw[a][:, j0 : j0 + HALF], tabw[a][:].indirect(idx[:, j0 // 16 : (j0 + HALF) // 16]))
 
-        w2s = tile([P, H], U8, "w2s", tag="w1_bf0")
-        nc.vector.tensor_copy(w2s[:].rearrange("p (t m) -> p t m", t=PACK), w2s_raw[:].rearrange("p (m t) -> p t m", t=PACK))
         page = {}
         page0_rows = page0.rearrange("(p t) m -> t p m", t=PACK)
         wgs_rows = wgs.rearrange("(q t) j -> q t j", t=PACK)
         wgs_t = {}
 
-        def load_wgs(half, t0, t1, tag):
-            part = tile([P, t1 - t0, HALF], F32, "wgs%d_%d" % (half, t0), tag=tag)
+        def load_wgs(j0, n, t0, t1, tag):
+            part = tile([P, t1 - t0, n], F32, "wgs%d_%d" % (j0, t0), tag=tag)
             for q in QUADRANT_ORDER:
-                nc.sync.dma_start(part[32 * q : 32 * q + 32], wgs_rows[:, t0:t1, half * HALF : (half + 1) * HALF])
+                nc.sync.dma_start(part[32 * q : 32 * q + 32], wgs_rows[:, t0:t1, j0 : j0 + n])
             for t in range(t0, t1):
-                wgs_t[half, t] = part[:, t - t0, :]
+                for j in range(0, n, 256):
+                    wgs_t[j0 + j, t] = part[:, t - t0, j:n]
 
         def load_page(t, tag):
             page[t] = tile([P, T2], F32, "page%d" % t, tag=tag)
             nc.sync.dma_start(page[t][:], page0_rows[t])
 
-        load_wgs(0, 0, 2, "w1_bf1")
-        load_page(0, "w2s_raw")
+        load_page(0, "w1_raw")
+        load_wgs(0, 256, 0, 2, "w1_bf1")
         load_page(1, "wide1")
 
         base, fur, rb, h, actc, acts, act_bf = {}, {}, {}, {}, {}, {}, {}
@@ -156,7 +157,8 @@ def tile_list_rubric_prefix_cache_kernel(
                 nc.scalar.activation(rows[:, t, :], gs[t][:], COPY, scale=gain_t[:, t : t + 1])
             act_bf[c] = tile([P, n * PACK], BF16, "act_bf%d" % c, tag="hold%d" % c)
             nc.scalar.copy(
-                act_bf[c][:].rearrange("p (n t) -> p n t", t=PACK), rows[:].rearrange("p t n -> p n t")
+                act_bf[c][:].rearrange("p (g i t) -> p g t i", i=4, t=PACK),
+                rows[:].rearrange("p t (g i) -> p g t i", i=4),
             )
 
         def quant_act(c):
@@ -183,7 +185,7 @@ def tile_list_rubric_prefix_cache_kernel(
             nc.vector.tensor_tensor(dst, fur[c, t], rb[c, t], ADD)
 
         def scatter_span(t, j0, n, values):
-            weights = wgs_t[j0 // HALF, t][:, j0 % HALF : j0 % HALF + n]
+            weights = wgs_t[j0, t][:, 0:n]
             nc.vector.tensor_tensor(page[t][:].indirect(idx2[:, j0 // 16 : (j0 + n) // 16]), values, weights, MULT)
 
         def scatter(c, t):
@@ -205,10 +207,10 @@ def tile_list_rubric_prefix_cache_kernel(
                 act_bf[0][:].rearrange("p (n t) -> p t n", t=PACK)[:, t, :], g[:], gain_t[:, t : t + 1], None, MULT
             )
         quant_act(0)
-        load_wgs(0, 2, 4, "g0_0")
-        load_page(2, "g0_1")
-        load_page(3, "g0_2")
-        load_wgs(1, 0, 4, "g0_3")
+        load_wgs(256, 256, 0, 2, "g0_0")
+        load_wgs(0, HALF, 2, 4, "g0_1")
+        load_page(2, "g0_2")
+        load_page(3, "g0_3")
         for t in range(2):
             residual(0, t)
             mm2(0, t, t)
@@ -219,6 +221,7 @@ def tile_list_rubric_prefix_cache_kernel(
                 for a in range(PASSES):
                     mm1(1, t, a)
         add(0, 0, h_tile(0, 0))
+        load_wgs(HALF, HALF, 0, 4, "rb0_0")
         add(0, 1, h_tile(0, 1))
         scatter(0, 0)
         scatter(0, 1)
@@ -308,7 +311,8 @@ def tile_list_rubric_prefix_cache_kernel(
             round_page(k, PACK - 1)
             page_bf = tile([P, w * PACK], BF16, "page_bf%d" % k, tag="page_bf", bufs=3)
             (nc.vector.tensor_copy if k < 2 else nc.scalar.copy)(
-                page_bf[:].rearrange("p (m t) -> p m t", t=PACK), rounded[k][:].rearrange("p t m -> p m t")
+                page_bf[:].rearrange("p (g i t) -> p g t i", i=4, t=PACK),
+                rounded[k][:].rearrange("p t (g i) -> p g t i", i=4),
             )
             if k < 2:
                 pcode[k] = pcode_head[:, m0 : m0 + w]

@@ -23,10 +23,20 @@ P = 128
 PACK = 4
 PASSES = K // (P * PACK)
 BANK = 512
+BANKS = 8
+QUAD = 32
+SCALE_ROWS = 4
+PER_COLUMN = 16
 HALF = S // 2
-TOKEN_CHUNKS = ((0, 256), (256, 256), (512, 512))
-PAGE_CHUNKS = ((0, 256), (256, 256), (512, 512), (1024, 512), (1536, 512))
+SHORT = 256
+TOKEN_CHUNKS = ((0, SHORT), (SHORT, SHORT), (HALF, HALF))
+PAGE_CHUNKS = ((0, 256), (256, 512), (768, 512), (1280, 512), (1792, 256))
+VECTOR_PAGE_CHUNKS = 2
+W1_VECTOR_GROUPS = (P, 40)
 QUADRANT_ORDER = (0, 2, 1, 3)
+RUN = 4
+GELU_BUFS = PACK
+WOVEN_BUFS = 3
 
 
 def tile_list_rubric_prefix_cache_kernel(
@@ -38,322 +48,339 @@ def tile_list_rubric_prefix_cache_kernel(
         lists = ctx.enter_context(tc.tile_pool(name="lists", bufs=1))
         sb = ctx.enter_context(tc.tile_pool(name="sb", bufs=1))
         psum = ctx.enter_context(tc.psum_pool(name="psum", bufs=1))
+        slot_of = {}
 
-        def tile(shape, dtype, name, tag=None, bufs=1):
-            return sb.tile(shape, dtype, name=name, tag=tag or name, bufs=bufs, align_bytes=64)
+        def tile(shape, dtype, name, after=None):
+            slot_of[name] = name if after is None else slot_of[after]
+            return sb.tile(shape, dtype, name=name, tag=slot_of[name], bufs=1, align_bytes=64)
+
+        def ring_tile(shape, dtype, name, ring, bufs):
+            return sb.tile(shape, dtype, name=name, tag=ring, bufs=bufs, align_bytes=64)
 
         def bank(index, name):
             return psum.tile([P, BANK], F32, name=name, tag="bank%d" % index)
 
-        idx = lists.tile([P, S // 16], U16, name="idx")
-        idx2 = lists.tile([P, S // 16], U16, name="idx2")
-        w2w_raw = tile([P, 2 * H], U8, "w2w_raw")
-        nc.sync.dma_start(w2w_raw[:].bitcast(I32), w2_words[0].bitcast(I32))
+        def offsets(list_tile, j0, n):
+            return list_tile[:, j0 // PER_COLUMN : (j0 + n) // PER_COLUMN]
+
+        def weave(copy, woven, slices):
+            copy(
+                woven.rearrange("p (g i t) -> p g t i", i=RUN, t=PACK),
+                slices.rearrange("p t (g i) -> p g t i", i=RUN),
+            )
+
+        def quantize(codes, scales, woven):
+            nc.vector.quantize_mx(out=codes.bitcast(FP8X4), scales=scales, in_=woven)
+
+        idx = lists.tile([P, S // PER_COLUMN], U16, name="idx")
+        idx2 = lists.tile([P, S // PER_COLUMN], U16, name="idx2")
+        w2_words_raw = [tile([P, H], U8, "w2_words_raw%d" % u) for u in range(2)]
+        for u in range(2):
+            nc.sync.dma_start(w2_words_raw[u][:].bitcast(I32), w2_words[0, :, u * H : (u + 1) * H].bitcast(I32))
         nc.sync.dma_start(idx[:], offs)
-        w1_raw = tile([P, PASSES, PACK, H], F32, "w1_raw")
-        nc.sync.dma_start(w1_raw[:], w1.rearrange("(a p j) r -> p a j r", a=PASSES, j=PACK))
         nc.sync.dma_start(idx2[:], offs2)
-        tabw = [tile([P, T], U32, "tabw%d" % a, tag="wide%d" % a) for a in range(PASSES)]
+        gain_sb = tile([P, PACK], F32, "gain_sb")
+        res_sb = tile([P, PACK], F32, "res_sb")
+        nc.scalar.dma_start(gain_sb[:], gain.rearrange("(p t) -> p t", t=PACK))
+        nc.scalar.dma_start(res_sb[:], res.rearrange("(p t) -> p t", t=PACK))
+        w1_raw = tile([P, PASSES, PACK, H], F32, "w1_raw")
+        nc.sync.dma_start(w1_raw[:], w1.rearrange("(a p i) r -> p a i r", a=PASSES, i=PACK))
+
+        tab_scales_sb = tile([P, T], U8, "tab_scales_sb")
+        nc.vector.memset(tab_scales_sb[:].bitcast(I32), 0)
+        for q in QUADRANT_ORDER:
+            nc.sync.dma_start(
+                tab_scales_sb[QUAD * q : QUAD * q + SCALE_ROWS * PASSES, :].bitcast(I32),
+                tab_scales[:, SCALE_ROWS * q : SCALE_ROWS * (q + 1), :].bitcast(I32),
+            )
+
+        w2_codes = tile([P, 2 * H], U8, "w2_codes")
+        for u in range(2):
+            nc.vector.tensor_copy(
+                w2_codes[:].rearrange("p (t m b) -> p t m b", t=PACK, b=2)[:, :, u * P // 2 : (u + 1) * P // 2, :],
+                w2_words_raw[u][:].rearrange("p (m t b) -> p t m b", t=PACK, b=2),
+            )
+        tab_words_sb = {}
+
+        def load_table_words(a, after):
+            tab_words_sb[a] = tile([P, T], U32, "tab_words_sb%d" % a, after=after)
+            nc.sync.dma_start(tab_words_sb[a][:].bitcast(I32), tab_words[a].rearrange("p t i -> p (t i)").bitcast(I32))
+
+        load_table_words(0, after="w2_words_raw0")
+        w2_scales_raw = tile([P, H], U8, "w2_scales_raw", after="w2_words_raw1")
+        nc.vector.memset(w2_scales_raw[:].bitcast(I32), 0)
+        for q in QUADRANT_ORDER:
+            nc.sync.dma_start(
+                w2_scales_raw[QUAD * q : QUAD * q + SCALE_ROWS, :].bitcast(I32),
+                w2_scales[0, SCALE_ROWS * q : SCALE_ROWS * (q + 1), :].bitcast(I32),
+            )
+
+        w1_codes = [tile([P, H], U32, "w1_codes%d" % a) for a in range(PASSES)]
+        w1_scales = [tile([P, H], U8, "w1_scales%d" % a) for a in range(PASSES)]
         for a in range(PASSES):
-            nc.sync.dma_start(tabw[a][:].bitcast(I32), tab_words[a].rearrange("p t i -> p (t i)").bitcast(I32))
-
-        tabs = tile([P, T], U8, "tabs")
-        nc.vector.memset(tabs[:].bitcast(I32), 0)
-        for a in range(PASSES):
-            for q in QUADRANT_ORDER:
-                (nc.scalar, nc.gpsimd)[a].dma_start(
-                    tabs[32 * q + 4 * a : 32 * q + 4 * a + 4, :].bitcast(I32), tab_scales[a, 4 * q : 4 * q + 4, :].bitcast(I32)
-                )
-
-        w2s_raw = tile([P, H], U8, "w2s_raw")
-        gain_t = tile([P, PACK], F32, "gain_t")
-        res_t = tile([P, PACK], F32, "res_t")
-        nc.vector.memset(w2s_raw[:].bitcast(I32), 0)
-        for q in range(4):
-            nc.gpsimd.dma_start(w2s_raw[32 * q : 32 * q + 4, :].bitcast(I32), w2_scales[0, 4 * q : 4 * q + 4, :].bitcast(I32))
-        nc.gpsimd.dma_start(gain_t[:], gain.rearrange("(p t) -> p t", t=PACK))
-        nc.gpsimd.dma_start(res_t[:], res.rearrange("(p t) -> p t", t=PACK))
-
-        w2w = tile([P, 2 * H], U8, "w2w")
-        nc.vector.tensor_copy(
-            w2w[:].rearrange("p (t m b) -> p t m b", t=PACK, b=2), w2w_raw[:].rearrange("p (m t b) -> p t m b", t=PACK, b=2)
-        )
-
-        w1c = [tile([P, H], U32, "w1c%d" % a) for a in range(PASSES)]
-        w1s = [tile([P, H], U8, "w1s%d" % a) for a in range(PASSES)]
-        for a in range(PASSES):
-            w1_bf = tile([P, H * PACK], BF16, "w1_bf%d" % a)
-            dealt = w1_bf[:].rearrange("p (t m j) -> p m t j", t=PACK, j=PACK)
-            rows = w1_raw[:, a].rearrange("p j (m t) -> p m t j", t=PACK)
-            cut = (P, 40)[a]
+            w1_woven = tile([P, H * PACK], BF16, "w1_woven%d" % a)
+            dealt = w1_woven[:].rearrange("p (t m i) -> p m t i", t=PACK, i=PACK)
+            rows = w1_raw[:, a].rearrange("p i (m t) -> p m t i", t=PACK)
+            cut = W1_VECTOR_GROUPS[a]
             nc.vector.tensor_copy(dealt[:, 0:cut], rows[:, 0:cut])
             if cut < P:
                 nc.scalar.copy(dealt[:, cut:P], rows[:, cut:P])
-            nc.vector.quantize_mx(out=w1c[a][:].bitcast(FP8X4), scales=w1s[a][:], in_=w1_bf[:])
+            quantize(w1_codes[a][:], w1_scales[a][:], w1_woven[:])
 
-        w2s = tile([P, H], U8, "w2s", tag="w1_bf0")
-        nc.vector.tensor_copy(w2s[:].rearrange("p (t m) -> p t m", t=PACK), w2s_raw[:].rearrange("p (m t) -> p t m", t=PACK))
+        load_table_words(1, after="w1_raw")
 
-        vs = tile([P, S], U8, "vs", tag="w2s_raw")
-        nc.vector.tensor_copy(vs[:], tabs[:].indirect(idx[:]))
-        vw = {}
+        v_scales = tile([P, S], U8, "v_scales")
+        nc.vector.tensor_copy(v_scales[:], tab_scales_sb[:].indirect(idx[:]))
+        v_codes = {}
         for a in range(PASSES):
-            vw[a] = tile([P, S], U32, "vw%d" % a, tag=("tabs", "wide0")[a])
+            v_codes[a] = tile([P, S], U32, "v_codes%d" % a, after=("tab_scales_sb", "tab_words_sb0")[a])
             for j0 in (0, HALF):
-                nc.vector.tensor_copy(vw[a][:, j0 : j0 + HALF], tabw[a][:].indirect(idx[:, j0 // 16 : (j0 + HALF) // 16]))
+                nc.vector.tensor_copy(v_codes[a][:, j0 : j0 + HALF], tab_words_sb[a][:].indirect(offsets(idx, j0, HALF)))
+
+        w2_scales_sb = tile([P, H], U8, "w2_scales_sb")
+        nc.vector.tensor_copy(
+            w2_scales_sb[:].rearrange("p (t m) -> p t m", t=PACK), w2_scales_raw[:].rearrange("p (m t) -> p t m", t=PACK)
+        )
 
         page = {}
-        page0_rows = page0.rearrange("(p t) m -> t p m", t=PACK)
-        wgs_rows = wgs.rearrange("(q t) j -> q t j", t=PACK)
-        wgs_t = {}
+        page0_slices = page0.rearrange("(p t) m -> t p m", t=PACK)
+        wgs_slices = wgs.rearrange("(q t) j -> q t j", t=PACK)
+        wgs_from = {}
 
-        def load_wgs(j0, n, t0, t1, tag):
-            part = tile([P, t1 - t0, n], F32, "wgs%d_%d" % (j0, t0), tag=tag)
+        def load_wgs(j0, n, t0, t1, after):
+            piece = tile([P, t1 - t0, n], F32, "wgs%d_%d" % (j0, t0), after=after)
             for q in QUADRANT_ORDER:
-                nc.sync.dma_start(part[32 * q : 32 * q + 32], wgs_rows[:, t0:t1, j0 : j0 + n])
+                nc.sync.dma_start(piece[QUAD * q : QUAD * (q + 1)], wgs_slices[:, t0:t1, j0 : j0 + n])
             for t in range(t0, t1):
-                for j in range(0, n, 256):
-                    wgs_t[j0 + j, t] = part[:, t - t0, j:n]
+                for j in range(0, n, SHORT):
+                    wgs_from[j0 + j, t] = piece[:, t - t0, j:n]
 
-        def load_page(t, tag):
-            page[t] = tile([P, T2], F32, "page%d" % t, tag=tag)
-            nc.sync.dma_start(page[t][:], page0_rows[t])
+        def load_page(t, after):
+            page[t] = tile([P, T2], F32, "page%d" % t, after=after)
+            nc.sync.dma_start(page[t][:], page0_slices[t])
 
-        load_page(0, "w1_raw")
-        load_wgs(0, 256, 0, 2, "w1_bf1")
-        load_page(1, "wide1")
+        load_page(0, after="w1_woven1")
+        load_wgs(0, SHORT, 0, 2, after="w2_scales_raw")
+        load_page(1, after="tab_words_sb1")
 
-        base, fur, rb, h, actc, acts, act_bf = {}, {}, {}, {}, {}, {}, {}
+        base, further, res_base, h = {}, {}, {}, {}
+        act_woven, act_codes, act_scales = {}, {}, {}
 
-        def mm1(c, t, a):
+        def first_product(c, t, a):
             j0, n = TOKEN_CHUNKS[c]
             cols = slice(t * P, (t + 1) * P)
             nc.tensor.matmul_mx(
                 out=base[c, t],
-                lhsT=w1c[a][:, cols].bitcast(FP8X4),
-                lhsT_scale=w1s[a][:, cols],
-                rhs=vw[a][:, j0 : j0 + n].bitcast(FP8X4),
-                rhs_scale=vs[4 * a : P, j0 : j0 + n],
+                lhsT=w1_codes[a][:, cols].bitcast(FP8X4),
+                lhsT_scale=w1_scales[a][:, cols],
+                rhs=v_codes[a][:, j0 : j0 + n].bitcast(FP8X4),
+                rhs_scale=v_scales[SCALE_ROWS * a : P, j0 : j0 + n],
                 start=(a == 0),
                 stop=(a == PASSES - 1),
             )
 
-        def gelu(c, t):
-            n = TOKEN_CHUNKS[c][1]
-            g = tile([P, n], F32, "g%d_%d" % (c, t), tag="g" if c else None, bufs=4 if c else 1)
-            nc.scalar.activation(g[:], base[c, t], GELU)
-            return g
-
-        def residual(c, t, dst=None):
-            n = TOKEN_CHUNKS[c][1]
-            rb[c, t] = tile([P, n], F32, "rb%d_%d" % (c, t))[:] if dst is None else dst
-            nc.scalar.activation(rb[c, t], base[c, t], COPY, scale=res_t[:, t : t + 1])
+        def scale_base(c, t, dst=None):
+            if dst is None:
+                dst = tile([P, TOKEN_CHUNKS[c][1]], F32, "res_base%d_%d" % (c, t))[:]
+            res_base[c, t] = dst
+            nc.scalar.activation(dst, base[c, t], COPY, scale=res_sb[:, t : t + 1])
 
         def act_on_scalar(c):
             n = TOKEN_CHUNKS[c][1]
-            rows = tile([P, PACK, n], BF16, "act_rows%d" % c, tag="act_rows")
-            gs = [gelu(c, t) for t in range(PACK)]
+            act_slices = ring_tile([P, PACK, n], BF16, "act_slices%d" % c, "act_slices", 1)
+            gelus = []
             for t in range(PACK):
-                nc.scalar.activation(rows[:, t, :], gs[t][:], COPY, scale=gain_t[:, t : t + 1])
-            act_bf[c] = tile([P, n * PACK], BF16, "act_bf%d" % c, tag="hold%d" % c)
-            nc.scalar.copy(
-                act_bf[c][:].rearrange("p (g i t) -> p g t i", i=4, t=PACK),
-                rows[:].rearrange("p t (g i) -> p g t i", i=4),
-            )
+                gelus.append(ring_tile([P, n], F32, "gelu%d_%d" % (c, t), "gelu", GELU_BUFS))
+                nc.scalar.activation(gelus[t][:], base[c, t], GELU)
+            for t in range(PACK):
+                nc.scalar.activation(act_slices[:, t, :], gelus[t][:], COPY, scale=gain_sb[:, t : t + 1])
+            act_woven[c] = tile([P, n * PACK], BF16, "act_woven%d" % c)
+            weave(nc.scalar.copy, act_woven[c][:], act_slices[:])
 
-        def quant_act(c):
+        def quantize_act(c):
             n = TOKEN_CHUNKS[c][1]
-            actc[c] = tile([P, n], U32, "actc%d" % c)
-            acts[c] = tile([P, n], U8, "acts%d" % c)
-            nc.vector.quantize_mx(out=actc[c][:].bitcast(FP8X4), scales=acts[c][:], in_=act_bf[c][:])
+            act_codes[c] = tile([P, n], U32, "act_codes%d" % c)
+            act_scales[c] = tile([P, n], U8, "act_scales%d" % c)
+            quantize(act_codes[c][:], act_scales[c][:], act_woven[c][:])
 
-        def mm2(c, t, b):
+        def second_product(c, t, bank_index):
             n = TOKEN_CHUNKS[c][1]
-            fur[c, t] = bank(b, "fur%d_%d" % (c, t))[:, 0:n]
+            further[c, t] = bank(bank_index, "further%d_%d" % (c, t))[:, 0:n]
             nc.tensor.matmul_mx(
-                out=fur[c, t],
-                lhsT=w2w[:, 2 * t * P : 2 * (t + 1) * P].bitcast(FP4X4),
-                lhsT_scale=w2s[:, t * P : (t + 1) * P],
-                rhs=actc[c][:].bitcast(FP8X4),
-                rhs_scale=acts[c][:],
+                out=further[c, t],
+                lhsT=w2_codes[:, 2 * t * P : 2 * (t + 1) * P].bitcast(FP4X4),
+                lhsT_scale=w2_scales_sb[:, t * P : (t + 1) * P],
+                rhs=act_codes[c][:].bitcast(FP8X4),
+                rhs_scale=act_scales[c][:],
                 start=True,
                 stop=True,
             )
 
-        def add(c, t, dst):
+        def add_h(c, t, dst=None, after=None):
+            if dst is None:
+                dst = tile([P, TOKEN_CHUNKS[c][1]], F32, "h%d_%d" % (c, t), after=after)[:]
             h[c, t] = dst
-            nc.vector.tensor_tensor(dst, fur[c, t], rb[c, t], ADD)
+            nc.vector.tensor_tensor(dst, further[c, t], res_base[c, t], ADD)
 
-        def scatter_span(t, j0, n, values):
-            weights = wgs_t[j0, t][:, 0:n]
-            nc.vector.tensor_tensor(page[t][:].indirect(idx2[:, j0 // 16 : (j0 + n) // 16]), values, weights, MULT)
+        def scatter_tokens(t, j0, n, values):
+            nc.vector.tensor_tensor(page[t][:].indirect(offsets(idx2, j0, n)), values, wgs_from[j0, t][:, 0:n], MULT)
 
         def scatter(c, t):
             j0, n = TOKEN_CHUNKS[c]
-            scatter_span(t, j0, n, h[c, t])
-
-        def h_tile(c, t, tag=None):
-            return tile([P, TOKEN_CHUNKS[c][1]], F32, "h%d_%d" % (c, t), tag=tag)[:]
+            scatter_tokens(t, j0, n, h[c, t])
 
         for t in range(PACK):
-            base[0, t] = bank(t, "base0_%d" % t)[:, 0:256]
+            base[0, t] = bank(t, "base0_%d" % t)[:, 0:SHORT]
         for a in range(PASSES):
             for t in range(PACK):
-                mm1(0, t, a)
-        act_bf[0] = tile([P, 256 * PACK], BF16, "act_bf0")
+                first_product(0, t, a)
+        act_woven[0] = tile([P, SHORT * PACK], BF16, "act_woven0")
         for t in range(PACK):
-            g = gelu(0, t)
+            gelu0 = tile([P, SHORT], F32, "gelu0_%d" % t)
+            nc.scalar.activation(gelu0[:], base[0, t], GELU)
             nc.vector.tensor_scalar(
-                act_bf[0][:].rearrange("p (n t) -> p t n", t=PACK)[:, t, :], g[:], gain_t[:, t : t + 1], None, MULT
+                act_woven[0][:].rearrange("p (n t) -> p t n", t=PACK)[:, t, :], gelu0[:], gain_sb[:, t : t + 1], None, MULT
             )
-        quant_act(0)
-        load_wgs(256, 256, 0, 2, "g0_0")
-        load_wgs(0, HALF, 2, 4, "g0_1")
-        load_page(2, "g0_2")
-        load_page(3, "g0_3")
+        quantize_act(0)
+        load_wgs(SHORT, SHORT, 0, 2, after="gelu0_0")
+        load_wgs(0, HALF, 2, PACK, after="gelu0_1")
+        load_page(2, after="gelu0_2")
+        load_page(3, after="gelu0_3")
         for t in range(2):
-            residual(0, t)
-            mm2(0, t, t)
+            scale_base(0, t)
+            second_product(0, t, t)
+
         for pair in range(2):
             both = bank(4 + pair, "base1_%d" % pair)
             for t in (2 * pair, 2 * pair + 1):
-                base[1, t] = both[:, (t % 2) * 256 : (t % 2 + 1) * 256]
+                base[1, t] = both[:, (t % 2) * SHORT : (t % 2 + 1) * SHORT]
                 for a in range(PASSES):
-                    mm1(1, t, a)
-        add(0, 0, h_tile(0, 0))
-        load_wgs(HALF, HALF, 0, 4, "rb0_0")
-        add(0, 1, h_tile(0, 1))
+                    first_product(1, t, a)
+        add_h(0, 0)
+        load_wgs(HALF, HALF, 0, PACK, after="res_base0_0")
+        add_h(0, 1)
         scatter(0, 0)
         scatter(0, 1)
         act_on_scalar(1)
-        quant_act(1)
-        residual(1, 0)
-        residual(1, 1)
-        rb_late = tile([P, 2, 256], F32, "rb0_23", tag="act_bf0")
-        residual(0, 2, rb_late[:, 0, :])
-        residual(0, 3, rb_late[:, 1, :])
-        mm2(0, 2, 6)
-        mm2(0, 3, 7)
-        held = tile([P, 3, 256], F32, "h_held", tag="hold1")
-        add(0, 2, held[:, 0, :])
-        add(0, 3, held[:, 2, :])
-        mm2(1, 0, 4)
-        mm2(1, 1, 6)
+        quantize_act(1)
+        scale_base(1, 0)
+        scale_base(1, 1)
+        res_base_late = tile([P, 2, SHORT], F32, "res_base_late", after="act_woven0")
+        scale_base(0, 2, res_base_late[:, 0, :])
+        scale_base(0, 3, res_base_late[:, 1, :])
+        second_product(0, 2, 6)
+        second_product(0, 3, 7)
+        h_late = tile([P, 3, SHORT], F32, "h_late", after="act_woven1")
+        add_h(0, 2, dst=h_late[:, 0, :])
+        add_h(0, 3, dst=h_late[:, 2, :])
+        second_product(1, 0, 4)
+        second_product(1, 1, 6)
+
         for t in range(PACK):
             base[2, t] = bank(t, "base2_%d" % t)[:]
             for a in range(PASSES):
-                mm1(2, t, a)
-        w3_raw = tile([P, PACK, N], F32, "w3_raw", tag="tabs")
-        nc.sync.dma_start(w3_raw[:], w3.rearrange("(p j) n -> p j n", j=PACK))
-        add(1, 0, h_tile(1, 0))
-        add(1, 1, h_tile(1, 1))
+                first_product(2, t, a)
+        w3_raw = tile([P, PACK, N], F32, "w3_raw", after="v_codes0")
+        nc.sync.dma_start(w3_raw[:], w3.rearrange("(p i) n -> p i n", i=PACK))
+        add_h(1, 0)
+        add_h(1, 1)
         scatter(1, 0)
-        residual(1, 2)
-        mm2(1, 2, 4)
-        add(1, 2, held[:, 1, :])
+        scale_base(1, 2)
+        second_product(1, 2, 4)
+        add_h(1, 2, dst=h_late[:, 1, :])
         scatter(1, 1)
-        scatter_span(2, 0, HALF, held[:, 0:2, :].rearrange("p c n -> p (c n)"))
+        scatter_tokens(2, 0, HALF, h_late[:, 0:2, :].rearrange("p c n -> p (c n)"))
         scatter(0, 3)
         anchor_rows = anchor.rearrange("(j p) m -> p j m", p=P)
-        anc_tags = ("rb1_0", "rb1_1", "rb1_2", "h1_0", "h1_1")
-        anc = []
+        anchor_after = ("res_base1_0", "res_base1_1", "res_base1_2", "h1_0", "h1_1")
+        anchor_sb = []
         for k, (m0, w) in enumerate(PAGE_CHUNKS):
-            anc.append(tile([P, N // P, w], F32, "anc%d" % k, tag=anc_tags[k]))
-            nc.sync.dma_start(anc[k][:], anchor_rows[:, :, m0 : m0 + w])
+            anchor_sb.append(tile([P, N // P, w], F32, "anchor_sb%d" % k, after=anchor_after[k]))
+            nc.sync.dma_start(anchor_sb[k][:], anchor_rows[:, :, m0 : m0 + w])
         act_on_scalar(2)
-        quant_act(2)
-        residual(1, 3)
-        mm2(1, 3, 5)
-        add(1, 3, h_tile(1, 3, tag="hold2"))
+        quantize_act(2)
+        scale_base(1, 3)
+        second_product(1, 3, 5)
+        add_h(1, 3, after="act_woven2")
         for t in range(PACK):
-            residual(2, t)
-        for t in range(PACK):
-            mm2(2, t, (4, 6, 7, 5)[t])
-        add(2, 0, h_tile(2, 0))
-        add(2, 1, h_tile(2, 1))
+            scale_base(2, t)
+        for t, bank_index in enumerate((4, 6, 7, 5)):
+            second_product(2, t, bank_index)
+        add_h(2, 0)
+        add_h(2, 1)
         scatter(1, 3)
 
-        out1_rows = out_1.rearrange("(p t) m -> t p m", t=PACK)
+        out_1_slices = out_1.rearrange("(p t) m -> t p m", t=PACK)
         rounded = [tile([P, PACK, w], BF16, "rounded%d" % k) for k, (m0, w) in enumerate(PAGE_CHUNKS)]
-
-        def round_page(k, t):
-            m0, w = PAGE_CHUNKS[k]
-            nc.scalar.copy(rounded[k][:, t, :], page[t][:, m0 : m0 + w])
-
         for t in range(PACK):
             scatter(2, t)
             if t + 2 < PACK:
-                add(2, t + 2, h_tile(2, t + 2, tag="h2_%d" % (t + 2)))
-            nc.sync.dma_start(out1_rows[t], page[t][:])
-            if t < PACK - 1:
-                for k in range(len(PAGE_CHUNKS)):
-                    round_page(k, t)
+                add_h(2, t + 2)
+            nc.sync.dma_start(out_1_slices[t], page[t][:])
+            for k, (m0, w) in enumerate(PAGE_CHUNKS):
+                on_vector = k < VECTOR_PAGE_CHUNKS and t == PACK - 1
+                copy = nc.vector.tensor_copy if on_vector else nc.scalar.copy
+                copy(rounded[k][:, t, :], page[t][:, m0 : m0 + w])
             if t == 0:
-                w3_bf = tile([P, N * PACK], BF16, "w3_bf", tag="h2_0")
-                nc.scalar.copy(w3_bf[:].rearrange("p (n j) -> p n j", j=PACK), w3_raw[:].rearrange("p j n -> p n j"))
+                w3_woven = tile([P, N * PACK], BF16, "w3_woven", after="h2_0")
+                nc.scalar.copy(w3_woven[:].rearrange("p (n i) -> p n i", i=PACK), w3_raw[:].rearrange("p i n -> p n i"))
 
-        w3c = tile([P, N], U32, "w3c", tag="h2_3")
-        w3s = tile([P, N], U8, "w3s")
-        for n0, n1 in ((0, 256), (256, N)):
-            nc.vector.quantize_mx(
-                out=w3c[:, n0:n1].bitcast(FP8X4), scales=w3s[:, n0:n1], in_=w3_bf[:, n0 * PACK : n1 * PACK]
-            )
+        w3_codes = tile([P, N], U32, "w3_codes", after="h2_3")
+        w3_scales = tile([P, N], U8, "w3_scales")
+        for n0, n1 in ((0, 2 * P), (2 * P, N)):
+            quantize(w3_codes[:, n0:n1], w3_scales[:, n0:n1], w3_woven[:, n0 * PACK : n1 * PACK])
 
-        pscale = tile([P, T2], U8, "pscale")
-        out0_rows = out_0.rearrange("(j p) m -> p j m", p=P)
-        out2_words = out_2[0].rearrange("p m t -> p (m t)").bitcast(I32)
-        pcode = {}
-        pcode_head = tile([P, BANK], U32, "pcode_head")
-        feat_head = tile([P, N // P, BANK], F32, "feat_head")
+        page_scales = tile([P, T2], U8, "page_scales")
+        out_0_rows = out_0.rearrange("(j p) m -> p j m", p=P)
+        out_2_words = out_2[0].rearrange("p m t -> p (m t)").bitcast(I32)
+        last_chunk = len(PAGE_CHUNKS) - 1
+        head_columns = PAGE_CHUNKS[VECTOR_PAGE_CHUNKS][0]
+        head_codes = tile([P, head_columns], U32, "head_codes")
+        page_codes = {}
 
-        def quant_page(k):
+        def quantize_page(k):
             m0, w = PAGE_CHUNKS[k]
-            round_page(k, PACK - 1)
-            page_bf = tile([P, w * PACK], BF16, "page_bf%d" % k, tag="page_bf", bufs=3)
-            (nc.vector.tensor_copy if k < 2 else nc.scalar.copy)(
-                page_bf[:].rearrange("p (g i t) -> p g t i", i=4, t=PACK),
-                rounded[k][:].rearrange("p t (g i) -> p g t i", i=4),
-            )
-            if k < 2:
-                pcode[k] = pcode_head[:, m0 : m0 + w]
+            in_head = k < VECTOR_PAGE_CHUNKS
+            page_woven = ring_tile([P, w * PACK], BF16, "page_woven%d" % k, "page_woven", WOVEN_BUFS)
+            weave(nc.vector.tensor_copy if in_head else nc.scalar.copy, page_woven[:], rounded[k][:])
+            if in_head:
+                page_codes[k] = head_codes[:, m0 : m0 + w]
             else:
-                pcode[k] = tile([P, w], U32, "pcode%d" % k, tag=anc_tags[k - 2])[:]
-            nc.vector.quantize_mx(out=pcode[k].bitcast(FP8X4), scales=pscale[:, m0 : m0 + w], in_=page_bf[:])
-            if k == 1:
-                nc.sync.dma_start(out2_words[:, 0:BANK], pcode_head[:].bitcast(I32))
-            if k >= 2:
-                nc.sync.dma_start(out2_words[:, m0 : m0 + w], pcode[k].bitcast(I32))
+                page_codes[k] = tile([P, w], U32, "page_codes%d" % k, after="anchor_sb%d" % (k - 2))[:]
+            quantize(page_codes[k], page_scales[:, m0 : m0 + w], page_woven[:])
+            if k == VECTOR_PAGE_CHUNKS - 1:
+                nc.sync.dma_start(out_2_words[:, 0:head_columns], head_codes[:].bitcast(I32))
+            if not in_head:
+                nc.sync.dma_start(out_2_words[:, m0 : m0 + w], page_codes[k].bitcast(I32))
 
         def features(k):
             m0, w = PAGE_CHUNKS[k]
-            dst = feat_head[:, :, m0 : m0 + w] if k < 2 else tile([P, N // P, w], F32, "feat%d" % k)[:]
-            last = k == len(PAGE_CHUNKS) - 1
+            feat = tile([P, N // P, w], F32, "feat%d" % k)[:]
             for j in range(N // P):
-                y = bank((3 * k + j) % 8, "y%d_%d" % (k, j))[:, 0:w]
+                product = bank((N // P * k + j) % BANKS, "product%d_%d" % (k, j))[:, 0:w]
                 nc.tensor.matmul_mx(
-                    out=y,
-                    lhsT=w3c[:, j * P : (j + 1) * P].bitcast(FP8X4),
-                    lhsT_scale=w3s[:, j * P : (j + 1) * P],
-                    rhs=pcode[k].bitcast(FP8X4),
-                    rhs_scale=pscale[:, m0 : m0 + w],
+                    out=product,
+                    lhsT=w3_codes[:, j * P : (j + 1) * P].bitcast(FP8X4),
+                    lhsT_scale=w3_scales[:, j * P : (j + 1) * P],
+                    rhs=page_codes[k].bitcast(FP8X4),
+                    rhs_scale=page_scales[:, m0 : m0 + w],
                     start=True,
                     stop=True,
                 )
-                nc.vector.tensor_tensor(dst[:, j, :], y, anc[k][:, j, :], SUB)
-                if last:
-                    nc.sync.dma_start(out0_rows[:, j, m0 : m0 + w], dst[:, j, :])
-            if k == 1:
-                nc.sync.dma_start(out0_rows[:, :, 0:BANK], feat_head[:])
-            if k >= 2 and not last:
-                nc.sync.dma_start(out0_rows[:, :, m0 : m0 + w], dst)
+                nc.vector.tensor_tensor(feat[:, j, :], product, anchor_sb[k][:, j, :], SUB)
+                if k == last_chunk:
+                    nc.sync.dma_start(out_0_rows[:, j, m0 : m0 + w], feat[:, j, :])
+            if k < last_chunk:
+                nc.sync.dma_start(out_0_rows[:, :, m0 : m0 + w], feat)
 
-        quant_page(0)
+        quantize_page(0)
         for k in range(len(PAGE_CHUNKS)):
-            if k + 1 < len(PAGE_CHUNKS):
-                quant_page(k + 1)
-            if k + 2 == len(PAGE_CHUNKS):
-                for q in range(4):
+            if k < last_chunk:
+                quantize_page(k + 1)
+            if k + 1 == last_chunk:
+                for q in range(P // QUAD):
                     nc.sync.dma_start(
-                        out_3[0, 4 * q : 4 * q + 4, :].bitcast(I32), pscale[32 * q : 32 * q + 4, :].bitcast(I32)
+                        out_3[0, SCALE_ROWS * q : SCALE_ROWS * (q + 1), :].bitcast(I32),
+                        page_scales[QUAD * q : QUAD * q + SCALE_ROWS, :].bitcast(I32),
                     )
             features(k)

from contextlib import ExitStack

import concourse.mybir as mybir

K, T, S, T2, H, N = 1024, 4096, 1024, 2048, 512, 384
FLOPS = 2 * (K * H * S + H * H * S + H * N * T2)

F32 = mybir.dt.float32
BF16 = mybir.dt.bfloat16
I32 = mybir.dt.int32
U32 = mybir.dt.uint32
U16 = mybir.dt.uint16
U8 = mybir.dt.uint8
FP8X4 = mybir.dt.float8_e4m3fn_x4
FP4X4 = mybir.dt.float4_e2m1fn_x4
MULT = mybir.AluOpType.mult
ADD = mybir.AluOpType.add
SUB = mybir.AluOpType.subtract
GELU = mybir.ActivationFunctionType.Gelu_apprx_tanh
COPY = mybir.ActivationFunctionType.Copy

P = 128
PACK = 4
PASSES = K // (P * PACK)
BANK = 512
BANKS = 8
QUAD = 32
SCALE_ROWS = 4
PER_COLUMN = 16
HALF = S // 2
SHORT = 256
TOKEN_CHUNKS = ((0, SHORT), (SHORT, SHORT), (HALF, HALF))
PAGE_CHUNKS = ((0, 256), (256, 512), (768, 512), (1280, 512), (1792, 256))
VECTOR_PAGE_CHUNKS = 2
W1_VECTOR_GROUPS = (P, 40)
QUADRANT_ORDER = (0, 2, 1, 3)
RUN = 4
GELU_BUFS = PACK
WOVEN_BUFS = 3


def tile_list_rubric_prefix_cache_kernel(
    tc, tab_words, tab_scales, offs, offs2, w1, gain, w2_words, w2_scales, res, wgs, page0, w3, anchor,
    out_0, out_1, out_2, out_3,
):
    nc = tc.nc
    with ExitStack() as ctx:
        lists = ctx.enter_context(tc.tile_pool(name="lists", bufs=1))
        sb = ctx.enter_context(tc.tile_pool(name="sb", bufs=1))
        psum = ctx.enter_context(tc.psum_pool(name="psum", bufs=1))
        slot_of = {}

        def tile(shape, dtype, name, after=None):
            slot_of[name] = name if after is None else slot_of[after]
            return sb.tile(shape, dtype, name=name, tag=slot_of[name], bufs=1, align_bytes=64)

        def ring_tile(shape, dtype, name, ring, bufs):
            return sb.tile(shape, dtype, name=name, tag=ring, bufs=bufs, align_bytes=64)

        def bank(index, name):
            return psum.tile([P, BANK], F32, name=name, tag="bank%d" % index)

        def offsets(list_tile, j0, n):
            return list_tile[:, j0 // PER_COLUMN : (j0 + n) // PER_COLUMN]

        def weave(copy, woven, slices):
            copy(
                woven.rearrange("p (g i t) -> p g t i", i=RUN, t=PACK),
                slices.rearrange("p t (g i) -> p g t i", i=RUN),
            )

        def quantize(codes, scales, woven):
            nc.vector.quantize_mx(out=codes.bitcast(FP8X4), scales=scales, in_=woven)

        idx = lists.tile([P, S // PER_COLUMN], U16, name="idx")
        idx2 = lists.tile([P, S // PER_COLUMN], U16, name="idx2")
        w2_words_raw = [tile([P, H], U8, "w2_words_raw%d" % u) for u in range(2)]
        for u in range(2):
            nc.sync.dma_start(w2_words_raw[u][:].bitcast(I32), w2_words[0, :, u * H : (u + 1) * H].bitcast(I32))
        nc.sync.dma_start(idx[:], offs)
        nc.sync.dma_start(idx2[:], offs2)
        gain_sb = tile([P, PACK], F32, "gain_sb")
        res_sb = tile([P, PACK], F32, "res_sb")
        nc.scalar.dma_start(gain_sb[:], gain.rearrange("(p t) -> p t", t=PACK))
        nc.scalar.dma_start(res_sb[:], res.rearrange("(p t) -> p t", t=PACK))
        w1_raw = tile([P, PASSES, PACK, H], F32, "w1_raw")
        nc.sync.dma_start(w1_raw[:], w1.rearrange("(a p i) r -> p a i r", a=PASSES, i=PACK))

        tab_scales_sb = tile([P, T], U8, "tab_scales_sb")
        nc.vector.memset(tab_scales_sb[:].bitcast(I32), 0)
        for q in QUADRANT_ORDER:
            nc.sync.dma_start(
                tab_scales_sb[QUAD * q : QUAD * q + SCALE_ROWS * PASSES, :].bitcast(I32),
                tab_scales[:, SCALE_ROWS * q : SCALE_ROWS * (q + 1), :].bitcast(I32),
            )

        w2_codes = tile([P, 2 * H], U8, "w2_codes")
        for u in range(2):
            nc.vector.tensor_copy(
                w2_codes[:].rearrange("p (t m b) -> p t m b", t=PACK, b=2)[:, :, u * P // 2 : (u + 1) * P // 2, :],
                w2_words_raw[u][:].rearrange("p (m t b) -> p t m b", t=PACK, b=2),
            )
        tab_words_sb = {}

        def load_table_words(a, after):
            tab_words_sb[a] = tile([P, T], U32, "tab_words_sb%d" % a, after=after)
            nc.sync.dma_start(tab_words_sb[a][:].bitcast(I32), tab_words[a].rearrange("p t i -> p (t i)").bitcast(I32))

        load_table_words(0, after="w2_words_raw0")
        w2_scales_raw = tile([P, H], U8, "w2_scales_raw", after="w2_words_raw1")
        nc.vector.memset(w2_scales_raw[:].bitcast(I32), 0)
        for q in QUADRANT_ORDER:
            nc.sync.dma_start(
                w2_scales_raw[QUAD * q : QUAD * q + SCALE_ROWS, :].bitcast(I32),
                w2_scales[0, SCALE_ROWS * q : SCALE_ROWS * (q + 1), :].bitcast(I32),
            )

        w1_codes = [tile([P, H], U32, "w1_codes%d" % a) for a in range(PASSES)]
        w1_scales = [tile([P, H], U8, "w1_scales%d" % a) for a in range(PASSES)]
        for a in range(PASSES):
            w1_woven = tile([P, H * PACK], BF16, "w1_woven%d" % a)
            dealt = w1_woven[:].rearrange("p (t m i) -> p m t i", t=PACK, i=PACK)
            rows = w1_raw[:, a].rearrange("p i (m t) -> p m t i", t=PACK)
            cut = W1_VECTOR_GROUPS[a]
            nc.vector.tensor_copy(dealt[:, 0:cut], rows[:, 0:cut])
            if cut < P:
                nc.scalar.copy(dealt[:, cut:P], rows[:, cut:P])
            quantize(w1_codes[a][:], w1_scales[a][:], w1_woven[:])

        load_table_words(1, after="w1_raw")

        v_scales = tile([P, S], U8, "v_scales")
        nc.vector.tensor_copy(v_scales[:], tab_scales_sb[:].indirect(idx[:]))
        v_codes = {}
        for a in range(PASSES):
            v_codes[a] = tile([P, S], U32, "v_codes%d" % a, after=("tab_scales_sb", "tab_words_sb0")[a])
            for j0 in (0, HALF):
                nc.vector.tensor_copy(v_codes[a][:, j0 : j0 + HALF], tab_words_sb[a][:].indirect(offsets(idx, j0, HALF)))

        w2_scales_sb = tile([P, H], U8, "w2_scales_sb")
        nc.vector.tensor_copy(
            w2_scales_sb[:].rearrange("p (t m) -> p t m", t=PACK), w2_scales_raw[:].rearrange("p (m t) -> p t m", t=PACK)
        )

        page = {}
        page0_slices = page0.rearrange("(p t) m -> t p m", t=PACK)
        wgs_slices = wgs.rearrange("(q t) j -> q t j", t=PACK)
        wgs_from = {}

        def load_wgs(j0, n, t0, t1, after):
            piece = tile([P, t1 - t0, n], F32, "wgs%d_%d" % (j0, t0), after=after)
            for q in QUADRANT_ORDER:
                nc.sync.dma_start(piece[QUAD * q : QUAD * (q + 1)], wgs_slices[:, t0:t1, j0 : j0 + n])
            for t in range(t0, t1):
                for j in range(0, n, SHORT):
                    wgs_from[j0 + j, t] = piece[:, t - t0, j:n]

        def load_page(t, after):
            page[t] = tile([P, T2], F32, "page%d" % t, after=after)
            nc.sync.dma_start(page[t][:], page0_slices[t])

        load_page(0, after="w1_woven1")
        load_wgs(0, SHORT, 0, 2, after="w2_scales_raw")
        load_page(1, after="tab_words_sb1")

        base, further, res_base, h = {}, {}, {}, {}
        act_woven, act_codes, act_scales = {}, {}, {}

        def first_product(c, t, a):
            j0, n = TOKEN_CHUNKS[c]
            cols = slice(t * P, (t + 1) * P)
            nc.tensor.matmul_mx(
                out=base[c, t],
                lhsT=w1_codes[a][:, cols].bitcast(FP8X4),
                lhsT_scale=w1_scales[a][:, cols],
                rhs=v_codes[a][:, j0 : j0 + n].bitcast(FP8X4),
                rhs_scale=v_scales[SCALE_ROWS * a : P, j0 : j0 + n],
                start=(a == 0),
                stop=(a == PASSES - 1),
            )

        def scale_base(c, t, dst=None):
            if dst is None:
                dst = tile([P, TOKEN_CHUNKS[c][1]], F32, "res_base%d_%d" % (c, t))[:]
            res_base[c, t] = dst
            nc.scalar.activation(dst, base[c, t], COPY, scale=res_sb[:, t : t + 1])

        def act_on_scalar(c):
            n = TOKEN_CHUNKS[c][1]
            act_slices = ring_tile([P, PACK, n], BF16, "act_slices%d" % c, "act_slices", 1)
            gelus = []
            for t in range(PACK):
                gelus.append(ring_tile([P, n], F32, "gelu%d_%d" % (c, t), "gelu", GELU_BUFS))
                nc.scalar.activation(gelus[t][:], base[c, t], GELU)
            for t in range(PACK):
                nc.scalar.activation(act_slices[:, t, :], gelus[t][:], COPY, scale=gain_sb[:, t : t + 1])
            act_woven[c] = tile([P, n * PACK], BF16, "act_woven%d" % c)
            weave(nc.scalar.copy, act_woven[c][:], act_slices[:])

        def quantize_act(c):
            n = TOKEN_CHUNKS[c][1]
            act_codes[c] = tile([P, n], U32, "act_codes%d" % c)
            act_scales[c] = tile([P, n], U8, "act_scales%d" % c)
            quantize(act_codes[c][:], act_scales[c][:], act_woven[c][:])

        def second_product(c, t, bank_index):
            n = TOKEN_CHUNKS[c][1]
            further[c, t] = bank(bank_index, "further%d_%d" % (c, t))[:, 0:n]
            nc.tensor.matmul_mx(
                out=further[c, t],
                lhsT=w2_codes[:, 2 * t * P : 2 * (t + 1) * P].bitcast(FP4X4),
                lhsT_scale=w2_scales_sb[:, t * P : (t + 1) * P],
                rhs=act_codes[c][:].bitcast(FP8X4),
                rhs_scale=act_scales[c][:],
                start=True,
                stop=True,
            )

        def add_h(c, t, dst=None, after=None):
            if dst is None:
                dst = tile([P, TOKEN_CHUNKS[c][1]], F32, "h%d_%d" % (c, t), after=after)[:]
            h[c, t] = dst
            nc.vector.tensor_tensor(dst, further[c, t], res_base[c, t], ADD)

        def scatter_tokens(t, j0, n, values):
            nc.vector.tensor_tensor(page[t][:].indirect(offsets(idx2, j0, n)), values, wgs_from[j0, t][:, 0:n], MULT)

        def scatter(c, t):
            j0, n = TOKEN_CHUNKS[c]
            scatter_tokens(t, j0, n, h[c, t])

        for t in range(PACK):
            base[0, t] = bank(t, "base0_%d" % t)[:, 0:SHORT]
        for a in range(PASSES):
            for t in range(PACK):
                first_product(0, t, a)
        act_woven[0] = tile([P, SHORT * PACK], BF16, "act_woven0")
        for t in range(PACK):
            gelu0 = tile([P, SHORT], F32, "gelu0_%d" % t)
            nc.scalar.activation(gelu0[:], base[0, t], GELU)
            nc.vector.tensor_scalar(
                act_woven[0][:].rearrange("p (n t) -> p t n", t=PACK)[:, t, :], gelu0[:], gain_sb[:, t : t + 1], None, MULT
            )
        quantize_act(0)
        load_wgs(SHORT, SHORT, 0, 2, after="gelu0_0")
        load_wgs(0, HALF, 2, PACK, after="gelu0_1")
        load_page(2, after="gelu0_2")
        load_page(3, after="gelu0_3")
        for t in range(2):
            scale_base(0, t)
            second_product(0, t, t)

        for pair in range(2):
            both = bank(4 + pair, "base1_%d" % pair)
            for t in (2 * pair, 2 * pair + 1):
                base[1, t] = both[:, (t % 2) * SHORT : (t % 2 + 1) * SHORT]
                for a in range(PASSES):
                    first_product(1, t, a)
        add_h(0, 0)
        load_wgs(HALF, HALF, 0, PACK, after="res_base0_0")
        add_h(0, 1)
        scatter(0, 0)
        scatter(0, 1)
        act_on_scalar(1)
        quantize_act(1)
        scale_base(1, 0)
        scale_base(1, 1)
        res_base_late = tile([P, 2, SHORT], F32, "res_base_late", after="act_woven0")
        scale_base(0, 2, res_base_late[:, 0, :])
        scale_base(0, 3, res_base_late[:, 1, :])
        second_product(0, 2, 6)
        second_product(0, 3, 7)
        h_late = tile([P, 3, SHORT], F32, "h_late", after="act_woven1")
        add_h(0, 2, dst=h_late[:, 0, :])
        add_h(0, 3, dst=h_late[:, 2, :])
        second_product(1, 0, 4)
        second_product(1, 1, 6)

        for t in range(PACK):
            base[2, t] = bank(t, "base2_%d" % t)[:]
            for a in range(PASSES):
                first_product(2, t, a)
        w3_raw = tile([P, PACK, N], F32, "w3_raw", after="v_codes0")
        nc.sync.dma_start(w3_raw[:], w3.rearrange("(p i) n -> p i n", i=PACK))
        add_h(1, 0)
        add_h(1, 1)
        scatter(1, 0)
        scale_base(1, 2)
        second_product(1, 2, 4)
        add_h(1, 2, dst=h_late[:, 1, :])
        scatter(1, 1)
        scatter_tokens(2, 0, HALF, h_late[:, 0:2, :].rearrange("p c n -> p (c n)"))
        scatter(0, 3)
        anchor_rows = anchor.rearrange("(j p) m -> p j m", p=P)
        anchor_after = ("res_base1_0", "res_base1_1", "res_base1_2", "h1_0", "h1_1")
        anchor_sb = []
        for k, (m0, w) in enumerate(PAGE_CHUNKS):
            anchor_sb.append(tile([P, N // P, w], F32, "anchor_sb%d" % k, after=anchor_after[k]))
            nc.sync.dma_start(anchor_sb[k][:], anchor_rows[:, :, m0 : m0 + w])
        act_on_scalar(2)
        quantize_act(2)
        scale_base(1, 3)
        second_product(1, 3, 5)
        add_h(1, 3, after="act_woven2")
        for t in range(PACK):
            scale_base(2, t)
        for t, bank_index in enumerate((4, 6, 7, 5)):
            second_product(2, t, bank_index)
        add_h(2, 0)
        add_h(2, 1)
        scatter(1, 3)

        out_1_slices = out_1.rearrange("(p t) m -> t p m", t=PACK)
        rounded = [tile([P, PACK, w], BF16, "rounded%d" % k) for k, (m0, w) in enumerate(PAGE_CHUNKS)]
        for t in range(PACK):
            scatter(2, t)
            if t + 2 < PACK:
                add_h(2, t + 2)
            nc.sync.dma_start(out_1_slices[t], page[t][:])
            for k, (m0, w) in enumerate(PAGE_CHUNKS):
                on_vector = k < VECTOR_PAGE_CHUNKS and t == PACK - 1
                copy = nc.vector.tensor_copy if on_vector else nc.scalar.copy
                copy(rounded[k][:, t, :], page[t][:, m0 : m0 + w])
            if t == 0:
                w3_woven = tile([P, N * PACK], BF16, "w3_woven", after="h2_0")
                nc.scalar.copy(w3_woven[:].rearrange("p (n i) -> p n i", i=PACK), w3_raw[:].rearrange("p i n -> p n i"))

        w3_codes = tile([P, N], U32, "w3_codes", after="h2_3")
        w3_scales = tile([P, N], U8, "w3_scales")
        for n0, n1 in ((0, 2 * P), (2 * P, N)):
            quantize(w3_codes[:, n0:n1], w3_scales[:, n0:n1], w3_woven[:, n0 * PACK : n1 * PACK])

        page_scales = tile([P, T2], U8, "page_scales")
        out_0_rows = out_0.rearrange("(j p) m -> p j m", p=P)
        out_2_words = out_2[0].rearrange("p m t -> p (m t)").bitcast(I32)
        last_chunk = len(PAGE_CHUNKS) - 1
        head_columns = PAGE_CHUNKS[VECTOR_PAGE_CHUNKS][0]
        head_codes = tile([P, head_columns], U32, "head_codes")
        page_codes = {}

        def quantize_page(k):
            m0, w = PAGE_CHUNKS[k]
            in_head = k < VECTOR_PAGE_CHUNKS
            page_woven = ring_tile([P, w * PACK], BF16, "page_woven%d" % k, "page_woven", WOVEN_BUFS)
            weave(nc.vector.tensor_copy if in_head else nc.scalar.copy, page_woven[:], rounded[k][:])
            if in_head:
                page_codes[k] = head_codes[:, m0 : m0 + w]
            else:
                page_codes[k] = tile([P, w], U32, "page_codes%d" % k, after="anchor_sb%d" % (k - 2))[:]
            quantize(page_codes[k], page_scales[:, m0 : m0 + w], page_woven[:])
            if k == VECTOR_PAGE_CHUNKS - 1:
                nc.sync.dma_start(out_2_words[:, 0:head_columns], head_codes[:].bitcast(I32))
            if not in_head:
                nc.sync.dma_start(out_2_words[:, m0 : m0 + w], page_codes[k].bitcast(I32))

        def features(k):
            m0, w = PAGE_CHUNKS[k]
            feat = tile([P, N // P, w], F32, "feat%d" % k)[:]
            for j in range(N // P):
                product = bank((N // P * k + j) % BANKS, "product%d_%d" % (k, j))[:, 0:w]
                nc.tensor.matmul_mx(
                    out=product,
                    lhsT=w3_codes[:, j * P : (j + 1) * P].bitcast(FP8X4),
                    lhsT_scale=w3_scales[:, j * P : (j + 1) * P],
                    rhs=page_codes[k].bitcast(FP8X4),
                    rhs_scale=page_scales[:, m0 : m0 + w],
                    start=True,
                    stop=True,
                )
                nc.vector.tensor_tensor(feat[:, j, :], product, anchor_sb[k][:, j, :], SUB)
                if k == last_chunk:
                    nc.sync.dma_start(out_0_rows[:, j, m0 : m0 + w], feat[:, j, :])
            if k < last_chunk:
                nc.sync.dma_start(out_0_rows[:, :, m0 : m0 + w], feat)

        quantize_page(0)
        for k in range(len(PAGE_CHUNKS)):
            if k < last_chunk:
                quantize_page(k + 1)
            if k + 1 == last_chunk:
                for q in range(P // QUAD):
                    nc.sync.dma_start(
                        out_3[0, SCALE_ROWS * q : SCALE_ROWS * (q + 1), :].bitcast(I32),
                        page_scales[QUAD * q : QUAD * q + SCALE_ROWS, :].bitcast(I32),
                    )
            features(k)
